import numpy as np
import ml_dtypes


def mxq(x, axis, fmt="e4m3"):
    dtype, down = {"e4m3": (ml_dtypes.float8_e4m3fn, 7), "e5m2": (ml_dtypes.float8_e5m2, 14)}[fmt]
    v = np.moveaxis(np.asarray(x, np.float32).astype(ml_dtypes.bfloat16).astype(np.float64), axis, -1)
    blocks = v.reshape(v.shape[:-1] + (-1, 32))
    amax = np.abs(blocks).max(-1, keepdims=True)
    byte = np.maximum(np.where(amax > 0, np.frexp(amax)[1] - 1 + 127, 0) - down, 1)
    scale = np.exp2(byte - 127.0)
    codes = (blocks / scale).astype(np.float32).astype(dtype).astype(np.float64)
    return np.moveaxis((codes * scale).reshape(v.shape), -1, axis)


WIDE = False


def mx_kscale(k):
    if not WIDE:
        return np.ones(k)
    levels = np.array([10, -10, 5, -5, 0])
    if k % 512:
        return np.exp2(np.random.permutation(np.resize(levels, k // 32))).repeat(32)
    a = np.empty((k // 512, 16))
    for p in range(k // 512):
        a[p, :8] = np.random.permutation(np.resize(levels, 8))
        for g in range(8):
            far = levels[np.abs(levels - a[p, g]) >= 10]
            a[p, g + 8] = far[np.random.randint(len(far))]
    return np.exp2(a.ravel()).repeat(32)


def f64(x):
    return np.asarray(x).astype(np.float64)


def striped(idx):
    return np.tile(idx.reshape(-1, 16).T, (8, 1)).astype(np.uint16)


def unstriped(offs):
    return offs[:16].T.reshape(-1).astype(np.int64)


E2M1 = np.array([0.0, 0.5, 1.0, 1.5, 2.0, 3.0, 4.0, 6.0, -0.0, -0.5, -1.0, -1.5, -2.0, -3.0, -4.0, -6.0])


def pack_weight(w, fmt):
    k, n = w.shape
    w = f64(np.asarray(w, np.float32).astype(ml_dtypes.bfloat16)).reshape(k // 32, 32, n)
    amax = np.abs(w).max(1)
    if fmt == "e4m3":
        byte = np.frexp(amax)[1] - 1 + 127 - 7
    else:
        mant, ex = np.frexp(amax / 6.0)
        byte = np.where(mant > 0.5, ex, ex - 1) + 127
    byte = np.clip(np.where(amax > 0, byte, 1), 1, 254)
    scaled = (w * np.exp2(127.0 - byte)[:, None, :]).reshape(k, n).astype(np.float32)
    by_word = np.ascontiguousarray(scaled.reshape(k // 512, 128, 4, n).transpose(0, 1, 3, 2))
    if fmt == "e4m3":
        words = by_word.astype(ml_dtypes.float8_e4m3fn).view(np.uint8)
    else:
        c = by_word.astype(ml_dtypes.float4_e2m1fn).view(np.uint8) & 0xF
        words = (c[..., 0::2] | (c[..., 1::2] << 4)).reshape(k // 512, 128, 2 * n)
    return np.ascontiguousarray(words), np.ascontiguousarray(byte.astype(np.uint8).reshape(k // 512, 16, n))


def unpack_weight(words, scales, fmt):
    g, _, n = scales.shape
    words = np.ascontiguousarray(words).reshape(g, 128, n, -1)
    if fmt == "e4m3":
        vals = words.view(ml_dtypes.float8_e4m3fn).astype(np.float64)
    else:
        nib = np.empty((g, 128, n, 4), np.uint8)
        nib[..., 0::2] = words & 0xF
        nib[..., 1::2] = words >> 4
        vals = E2M1[nib]
    vals = vals * np.repeat(np.exp2(scales.astype(np.float64) - 127.0), 8, axis=1)[..., None]
    return vals.transpose(0, 1, 3, 2).reshape(g * 512, n)


def gelu(v):
    return 0.5 * v * (1.0 + np.tanh(np.sqrt(2.0 / np.pi) * (v + 0.044715 * v**3)))


def often(T, S):
    return np.random.permutation(T)[(T * np.random.uniform(0, 1, S) ** 4).astype(np.int64)]


K, T, T2, H, S, P, N = 1024, 4096, 2048, 1024, 1024, 512, 256

def setup_inputs():
    n = np.random.standard_normal
    s = mx_kscale(K)[:, None]
    u = mx_kscale(H)[:, None]
    tab_words, tab_scales = pack_weight(n((K, T)) * s, "e4m3")
    tab2_words, tab2_scales = pack_weight(n((K, T2)) * s, "e4m3")
    w1_words, w1_scales = pack_weight(2.5 * n((K, H)) / np.sqrt(K) / s, "e2m1")
    return {
        "tab_words": tab_words, "tab_scales": tab_scales,
        "offs": striped(np.random.permutation(T)[:S]),
        "w1_words": w1_words, "w1_scales": w1_scales,
        "pos1": striped(often(S, P)),
        "tab2_words": tab2_words, "tab2_scales": tab2_scales,
        "offs2": striped(np.random.permutation(T2)[:P]),
        "w2": (2.5 * n((K, H)) / np.sqrt(K) / s).astype(np.float32),
        "gain": (np.exp(0.3 * n(H)) * u[:, 0]).astype(np.float32),
        "w3": (1.5 * n((H, N)) / np.sqrt(H) / u).astype(np.float32),
    }

def reference(tab_words, tab_scales, offs, w1_words, w1_scales, pos1,
              tab2_words, tab2_scales, offs2, w2, gain, w3):
    v = unpack_weight(tab_words, tab_scales, "e4m3")[:, unstriped(offs)]
    v2 = unpack_weight(tab2_words, tab2_scales, "e4m3")[:, unstriped(offs2)]
    x1 = unpack_weight(w1_words, w1_scales, "e2m1").T @ v
    b = mxq(f64(w2), 0, "e4m3").T @ v2
    pe = 1.0 / (1.0 + np.exp(-x1[:, unstriped(pos1)]))
    pc = 1.0 / (1.0 + np.exp(-b))
    z = (pe + pc - 2.0 * pe * pc) * f64(gain)[:, None]
    return mxq(f64(w3), 0, "e4m3").T @ mxq(z, 0, "e4m3")

@@ -1,0 +1,272 @@
+from contextlib import ExitStack
+
+import concourse.mybir as mybir
+
+K, T, T2, H, S, M, N = 1024, 4096, 2048, 1024, 1024, 512, 256
+FLOPS = 2 * K * H * S + 2 * K * H * M + 2 * H * N * M
+
+F32 = mybir.dt.float32
+BF16 = mybir.dt.bfloat16
+I32 = mybir.dt.int32
+U32 = mybir.dt.uint32
+U16 = mybir.dt.uint16
+U8 = mybir.dt.uint8
+FP8X4 = mybir.dt.float8_e4m3fn_x4
+FP4X4 = mybir.dt.float4_e2m1fn_x4
+ACT = mybir.ActivationFunctionType
+ALU = mybir.AluOpType
+
+P = 128
+PACK = 4
+PASS = P * PACK
+BANK = 512
+OUT_PIECES = [(0, 256), (256, 512)]
+
+
+def tile_list_stemma_innovation_scores_kernel(
+    tc, tab_words, tab_scales, offs, w1_words, w1_scales, pos1,
+    tab2_words, tab2_scales, offs2, w2, gain, w3, out,
+):
+    nc = tc.nc
+    with ExitStack() as ctx:
+        lists = ctx.enter_context(tc.tile_pool(name="lists", bufs=1))
+        keep = ctx.enter_context(tc.tile_pool(name="keep", bufs=1))
+        ring = ctx.enter_context(tc.tile_pool(name="ring", bufs=4))
+        psum = ctx.enter_context(tc.psum_pool(name="psum", bufs=1))
+
+        def held(name, shape, dtype):
+            return keep.tile(shape, dtype, name=name, align_bytes=64)
+
+        def shared(name, tag, shape, dtype):
+            return keep.tile(shape, dtype, name=name, tag=tag, align_bytes=64)
+
+        tab_s = held("tab_s", [P, T], U8)
+        tab2_s = held("tab2_s", [P, T2], U8)
+        w1_s_raw = held("w1_s_raw", [P, H], U8)
+        warm = held("warm", [P, 2], F32)
+        nc.gpsimd.memset(warm[:], 0.0)
+        for rows in (tab_s, tab2_s, w1_s_raw):
+            nc.gpsimd.memset(rows[32:64, :].bitcast(I32), 0)
+            nc.vector.memset(rows[64:128, :].bitcast(I32), 0)
+        planes = [held("planes%d" % a, [P, S + H + M], U8) for a in range(2)]
+        nc.gpsimd.memset(planes[1][:].bitcast(I32), 0)
+        nc.scalar.activation(warm[:, 1:2], warm[:, 0:1], ACT.Tanh, scale=0.5)
+
+        idx = lists.tile([P, S // 16], U16, name="idx")
+        nc.sync.dma_start(idx[:], offs)
+        nc.sync.dma_start(tab_s[0:32, :].bitcast(I32), tab_scales.rearrange("a q t -> (a q) t").bitcast(I32))
+        idx2 = lists.tile([P, M // 16], U16, name="idx2")
+        nc.sync.dma_start(idx2[:], offs2)
+        nc.sync.dma_start(tab2_s[0:32, :].bitcast(I32), tab2_scales.rearrange("a q t -> (a q) t").bitcast(I32))
+        nc.sync.dma_start(w1_s_raw[0:32, :].bitcast(I32), w1_scales.rearrange("a q c -> (a q) c").bitcast(I32))
+        p1 = lists.tile([P, M // 16], U16, name="p1")
+        nc.sync.dma_start(p1[:], pos1)
+        w1_raw = shared("w1_raw", "mid1", [P, 4 * H], U8)
+        nc.sync.dma_start(
+            w1_raw[:].bitcast(I32).rearrange("p (a c) -> p a c", a=2),
+            w1_words.bitcast(I32).rearrange("a p c -> p a c"),
+        )
+        tab_w = []
+        for a in range(2):
+            tw = shared("tab_w%d" % a, "big%d" % a, [P, T], I32)
+            nc.sync.dma_start(tw[:], tab_words[a].rearrange("p t i -> p (t i)").bitcast(I32))
+            tab_w.append(tw)
+        gain_sb = held("gain_sb", [P, 2, PACK], F32)
+        nc.gpsimd.dma_start(gain_sb[:], gain.rearrange("(b p t) -> p b t", b=2, t=PACK))
+
+        v_s_got = shared("v_s_got", "mid0", [P, S], U8)
+        nc.vector.tensor_copy(v_s_got[:], tab_s[:].indirect(idx[:]))
+        v2_s_got = held("v2_s_got", [P, M], U8)
+        nc.vector.tensor_copy(v2_s_got[:], tab2_s[:].indirect(idx2[:]))
+        nc.vector.tensor_copy(
+            planes[0][:, S : S + H].rearrange("p (g t m) -> p g m t", t=PACK, m=P),
+            w1_s_raw[:].rearrange("p (g m t) -> p g m t", t=PACK, m=P),
+        )
+        nc.vector.tensor_copy(planes[0][:, :S].bitcast(I32), v_s_got[:].bitcast(I32))
+        nc.vector.tensor_copy(planes[0][:, S + H :].bitcast(I32), v2_s_got[:].bitcast(I32))
+        for a in range(2):
+            for q in range(1 - a, 4):
+                queue = nc.gpsimd if (a, q) == (0, 1) else nc.scalar
+                row = 16 * a + 4 * q
+                queue.dma_start(planes[a][32 * q : 32 * q + 4, :].bitcast(I32), planes[0][row : row + 4, :].bitcast(I32))
+
+        w1_c = held("w1_c", [P, 4 * H], U8)
+        nc.vector.tensor_copy(
+            w1_c[:].bitcast(U16).rearrange("p (g t m) -> p g m t", t=PACK, m=P),
+            w1_raw[:].bitcast(U16).rearrange("p (g m t) -> p g m t", t=PACK, m=P),
+        )
+        half_gain = held("half_gain", [P, 2, PACK], F32)
+        nc.vector.tensor_scalar(half_gain[:], gain_sb[:], 0.5, None, ALU.mult)
+        neg_half_gain = held("neg_half_gain", [P, 2, PACK], F32)
+        nc.vector.tensor_scalar(neg_half_gain[:], gain_sb[:], -0.5, None, ALU.mult)
+
+        v_c = {}
+        for a in range(2):
+            for h in range(2):
+                g = held("v_c%d%d" % (a, h), [P, BANK], U32)
+                nc.vector.tensor_copy(g[:], tab_w[a][:].bitcast(U32).indirect(idx[:, 32 * h : 32 * (h + 1)]))
+                v_c[a, h] = g
+
+        tab2_w = []
+        for a in range(2):
+            tw = shared("tab2_w%d" % a, "mid%d" % a, [P, T2], I32)
+            nc.sync.dma_start(tw[:], tab2_words[a].rearrange("p t i -> p (t i)").bitcast(I32))
+            tab2_w.append(tw)
+        w2_raw = {}
+        for b in range(2):
+            raw = shared("w2_raw%d" % b, "big%d" % b, [P, 2 * PACK * PASS], F32)
+            for a in range(2):
+                w2_raw[b, a] = raw[:, PACK * PASS * a : PACK * PASS * (a + 1)].rearrange("p (j c) -> p j c", j=PACK)
+                nc.sync.dma_start(
+                    w2_raw[b, a],
+                    w2[PASS * a : PASS * (a + 1), PASS * b : PASS * (b + 1)].rearrange("(p j) c -> p j c", j=PACK),
+                )
+        v2_c = []
+        for a in range(2):
+            g = held("v2_c%d" % a, [P, M], U32)
+            nc.vector.tensor_copy(g[:], tab2_w[a][:].bitcast(U32).indirect(idx2[:]))
+            v2_c.append(g)
+
+        w3_raw = []
+        for b in range(2):
+            raw = shared("w3_raw%d" % b, "mid%d" % b, [P, PACK, N], F32)
+            nc.sync.dma_start(raw[:], w3[PASS * b : PASS * (b + 1), :].rearrange("(p j) n -> p j n", j=PACK))
+            w3_raw.append(raw)
+
+        te = {}
+
+        def x1_half(b, t, h):
+            if (b, t) not in te:
+                te[b, t] = held("te%d%d" % (b, t), [P, S], F32)
+            acc = psum.tile([P, BANK], F32, name="acc", bufs=6)
+            for a in range(2):
+                c0 = H * a + PASS * b + P * t
+                nc.tensor.matmul_mx(
+                    out=acc[:],
+                    lhsT=w1_c[:, 2 * c0 : 2 * (c0 + P)].bitcast(FP4X4),
+                    lhsT_scale=planes[a][:, S + PASS * b + P * t : S + PASS * b + P * (t + 1)],
+                    rhs=v_c[a, h][:].bitcast(FP8X4),
+                    rhs_scale=planes[a][:, BANK * h : BANK * (h + 1)],
+                    start=(a == 0), stop=(a == 1),
+                )
+            nc.scalar.activation(te[b, t][:, BANK * h : BANK * (h + 1)], acc[:], ACT.Tanh, scale=0.5)
+
+        w2_c, w2_s, w2_b = {}, {}, {}
+
+        def w2_cast(b, a, copy):
+            wb = ring.tile([P, PACK, P, PACK], BF16, name="w2_b", align_bytes=64)
+            copy(wb[:].rearrange("p t m j -> p m j t"), w2_raw[b, a].rearrange("p j (m t) -> p m j t", t=PACK))
+            w2_b[b, a] = wb
+
+        def w2_quant(b, a):
+            w2_c[b, a] = held("w2_c%d%d" % (b, a), [P, PASS], U32)
+            w2_s[b, a] = held("w2_s%d%d" % (b, a), [P, PASS], U8)
+            nc.vector.quantize_mx(
+                out=w2_c[b, a][:].bitcast(FP8X4), scales=w2_s[b, a][:],
+                in_=w2_b[b, a][:].rearrange("p t m j -> p (t m j)"),
+            )
+
+        tcs = {}
+
+        def b_tile(b, t):
+            acc = psum.tile([P, M], F32, name="acc_b", bufs=2)
+            for a in range(2):
+                nc.tensor.matmul_mx(
+                    out=acc[:],
+                    lhsT=w2_c[b, a][:, P * t : P * (t + 1)].bitcast(FP8X4),
+                    lhsT_scale=w2_s[b, a][:, P * t : P * (t + 1)],
+                    rhs=v2_c[a][:].bitcast(FP8X4),
+                    rhs_scale=planes[a][:, S + H :],
+                    start=(a == 0), stop=(a == 1),
+                )
+            tcs[b, t] = ring.tile([P, M], F32, name="tc")
+            nc.scalar.activation(tcs[b, t][:], acc[:], ACT.Tanh, scale=0.5)
+
+        z_rows = {}
+
+        def xor_rows(b, t, m0, m1):
+            if (b, m0) not in z_rows:
+                z_rows[b, m0] = held("z_rows%d_%d" % (b, m0), [P, PACK, m1 - m0], BF16)
+            u = ring.tile([P, m1 - m0], F32, name="u")
+            nc.vector.tensor_tensor(u[:], te[b, t][:].indirect(p1[:, m0 // 16 : m1 // 16]), tcs[b, t][:, m0:m1], ALU.mult)
+            nc.scalar.activation(
+                z_rows[b, m0][:, t, :], u[:], ACT.Identity,
+                scale=neg_half_gain[:, b, t : t + 1], bias=half_gain[:, b, t : t + 1],
+            )
+
+        z_b = {}
+        z_c = [held("z_c%d" % b, [P, M], U32) for b in range(2)]
+        z_s = [held("z_s%d" % b, [P, M], U8) for b in range(2)]
+
+        def z_weave(b, m0, m1):
+            z_b[b, m0] = held("z_b%d_%d" % (b, m0), [P, m1 - m0, PACK], BF16)
+            nc.vector.tensor_copy(
+                z_b[b, m0][:].rearrange("p (c i) t -> p c t i", i=4),
+                z_rows[b, m0][:].rearrange("p t (c i) -> p c t i", i=4),
+            )
+
+        def z_quant(b, m0, m1):
+            nc.vector.quantize_mx(
+                out=z_c[b][:, m0:m1].bitcast(FP8X4), scales=z_s[b][:, m0:m1],
+                in_=z_b[b, m0][:].rearrange("p m t -> p (m t)"),
+            )
+
+        w3_c, w3_s = [], []
+
+        def w3_make(b):
+            wb = held("w3_b%d" % b, [P, N, PACK], BF16)
+            nc.vector.tensor_copy(
+                wb[:].rearrange("p (c i) j -> p c j i", i=4),
+                w3_raw[b][:].rearrange("p j (c i) -> p c j i", i=4),
+            )
+            w3_c.append(held("w3_c%d" % b, [P, N], U32))
+            w3_s.append(held("w3_s%d" % b, [P, N], U8))
+            nc.vector.quantize_mx(
+                out=w3_c[b][:].bitcast(FP8X4), scales=w3_s[b][:], in_=wb[:].rearrange("p n j -> p (n j)")
+            )
+
+        def out_piece(m0, m1):
+            for n in range(2):
+                acc = psum.tile([P, BANK], F32, name="acc", bufs=6)
+                for b in range(2):
+                    nc.tensor.matmul_mx(
+                        out=acc[:, : m1 - m0],
+                        lhsT=w3_c[b][:, P * n : P * (n + 1)].bitcast(FP8X4),
+                        lhsT_scale=w3_s[b][:, P * n : P * (n + 1)],
+                        rhs=z_c[b][:, m0:m1].bitcast(FP8X4),
+                        rhs_scale=z_s[b][:, m0:m1],
+                        start=(b == 0), stop=(b == 1),
+                    )
+                res = ring.tile([P, m1 - m0], F32, name="res")
+                copy = nc.vector.tensor_copy if (m1, n) == (M, 1) else nc.scalar.copy
+                copy(res[:], acc[:, : m1 - m0])
+                nc.sync.dma_start(out[P * n : P * (n + 1), m0:m1], res[:])
+
+        for t in range(PACK):
+            for h in range(2):
+                x1_half(0, t, h)
+        for a in range(2):
+            w2_cast(0, a, nc.vector.tensor_copy)
+        for a in range(2):
+            w2_quant(0, a)
+        for t in range(PACK):
+            b_tile(0, t)
+            xor_rows(0, t, 0, M)
+        for t in range(PACK):
+            for h in range(2):
+                x1_half(1, t, h)
+        for a in range(2):
+            w2_cast(1, a, nc.scalar.copy)
+            w2_quant(1, a)
+        z_weave(0, 0, M)
+        z_quant(0, 0, M)
+        for t in range(PACK):
+            b_tile(1, t)
+        for b in range(2):
+            w3_make(b)
+        for m0, m1 in OUT_PIECES:
+            for t in range(PACK):
+                xor_rows(1, t, m0, m1)
+            z_weave(1, m0, m1)
+            z_quant(1, m0, m1)
+            out_piece(m0, m1)

@@ -1,6 +1,7 @@
 from contextlib import ExitStack
 
 import concourse.mybir as mybir
+from concourse.masks import make_identity
 
 K, T, T2, H, S, M, N = 1024, 4096, 2048, 1024, 1024, 512, 256
 FLOPS = 2 * K * H * S + 2 * K * H * M + 2 * H * N * M
@@ -32,6 +33,7 @@ def tile_list_stemma_innovation_scores_kernel(
         lists = ctx.enter_context(tc.tile_pool(name="lists", bufs=1))
         keep = ctx.enter_context(tc.tile_pool(name="keep", bufs=1))
         ring = ctx.enter_context(tc.tile_pool(name="ring", bufs=4))
+        arena = ctx.enter_context(tc.tile_pool(name="arena", bufs=1))
         psum = ctx.enter_context(tc.psum_pool(name="psum", bufs=1))
 
         def held(name, shape, dtype):
@@ -40,16 +42,20 @@ def tile_list_stemma_innovation_scores_kernel(
         def shared(name, tag, shape, dtype):
             return keep.tile(shape, dtype, name=name, tag=tag, align_bytes=64)
 
+        def placed(name, kib, shape, dtype):
+            return arena.tile(shape, dtype, name=name, align_bytes=64, offset=int(1024 * kib))
+
         tab_s = held("tab_s", [P, T], U8)
         tab2_s = held("tab2_s", [P, T2], U8)
-        w1_s_raw = held("w1_s_raw", [P, H], U8)
+        w1_s_raw = held("w1_s_raw", [32, H], U8)
         warm = held("warm", [P, 2], F32)
         nc.gpsimd.memset(warm[:], 0.0)
-        for rows in (tab_s, tab2_s, w1_s_raw):
-            nc.gpsimd.memset(rows[32:64, :].bitcast(I32), 0)
+        for rows in (tab_s, tab2_s):
+            nc.vector.memset(rows[32:64, :].bitcast(I32), 0)
             nc.vector.memset(rows[64:128, :].bitcast(I32), 0)
         planes = [held("planes%d" % a, [P, S + H + M], U8) for a in range(2)]
-        nc.gpsimd.memset(planes[1][:].bitcast(I32), 0)
+        for a in range(2):
+            nc.gpsimd.memset(planes[a][:].bitcast(I32), 0)
         nc.scalar.activation(warm[:, 1:2], warm[:, 0:1], ACT.Tanh, scale=0.5)
 
         idx = lists.tile([P, S // 16], U16, name="idx")
@@ -61,77 +67,89 @@ def tile_list_stemma_innovation_scores_kernel(
         nc.sync.dma_start(w1_s_raw[0:32, :].bitcast(I32), w1_scales.rearrange("a q c -> (a q) c").bitcast(I32))
         p1 = lists.tile([P, M // 16], U16, name="p1")
         nc.sync.dma_start(p1[:], pos1)
-        w1_raw = shared("w1_raw", "mid1", [P, 4 * H], U8)
+        w1_raw = placed("w1_raw", 41, [P, 4 * H], U8)
         nc.sync.dma_start(
             w1_raw[:].bitcast(I32).rearrange("p (a c) -> p a c", a=2),
             w1_words.bitcast(I32).rearrange("a p c -> p a c"),
         )
         tab_w = []
         for a in range(2):
-            tw = shared("tab_w%d" % a, "big%d" % a, [P, T], I32)
+            tw = placed("tab_w%d" % a, (4, 25)[a], [P, T], I32)
             nc.sync.dma_start(tw[:], tab_words[a].rearrange("p t i -> p (t i)").bitcast(I32))
             tab_w.append(tw)
-        gain_sb = held("gain_sb", [P, 2, PACK], F32)
-        nc.gpsimd.dma_start(gain_sb[:], gain.rearrange("(b p t) -> p b t", b=2, t=PACK))
 
-        v_s_got = shared("v_s_got", "mid0", [P, S], U8)
+        v_s_got = held("v_s_got", [P, S], U8)
         nc.vector.tensor_copy(v_s_got[:], tab_s[:].indirect(idx[:]))
-        v2_s_got = held("v2_s_got", [P, M], U8)
+        v2_s_got = placed("v2_s_got", 52.75, [P, M], U8)
         nc.vector.tensor_copy(v2_s_got[:], tab2_s[:].indirect(idx2[:]))
+        nc.vector.tensor_copy(planes[0][0:32, :S].bitcast(I32), v_s_got[0:32, :].bitcast(I32))
         nc.vector.tensor_copy(
-            planes[0][:, S : S + H].rearrange("p (g t m) -> p g m t", t=PACK, m=P),
-            w1_s_raw[:].rearrange("p (g m t) -> p g m t", t=PACK, m=P),
+            planes[0][0:32, S : S + H].bitcast(I32).rearrange("p (b t g e) -> p b t g e", t=PACK, g=16, e=2),
+            w1_s_raw[:].bitcast(I32).rearrange("p (b g t e) -> p b t g e", t=PACK, g=16, e=2),
         )
-        nc.vector.tensor_copy(planes[0][:, :S].bitcast(I32), v_s_got[:].bitcast(I32))
-        nc.vector.tensor_copy(planes[0][:, S + H :].bitcast(I32), v2_s_got[:].bitcast(I32))
+        nc.vector.tensor_copy(planes[0][0:32, S + H :].bitcast(I32), v2_s_got[0:32, :].bitcast(I32))
         for a in range(2):
             for q in range(1 - a, 4):
                 queue = nc.gpsimd if (a, q) == (0, 1) else nc.scalar
                 row = 16 * a + 4 * q
                 queue.dma_start(planes[a][32 * q : 32 * q + 4, :].bitcast(I32), planes[0][row : row + 4, :].bitcast(I32))
 
-        w1_c = held("w1_c", [P, 4 * H], U8)
+        w1_c = placed("w1_c", 49, [P, 4 * H], U8)
         nc.vector.tensor_copy(
-            w1_c[:].bitcast(U16).rearrange("p (g t m) -> p g m t", t=PACK, m=P),
-            w1_raw[:].bitcast(U16).rearrange("p (g m t) -> p g m t", t=PACK, m=P),
+            w1_c[:].bitcast(I32).rearrange("p (b t g e) -> p b t g e", t=PACK, g=16, e=4),
+            w1_raw[:].bitcast(I32).rearrange("p (b g t e) -> p b t g e", t=PACK, g=16, e=4),
         )
-        half_gain = held("half_gain", [P, 2, PACK], F32)
-        nc.vector.tensor_scalar(half_gain[:], gain_sb[:], 0.5, None, ALU.mult)
-        neg_half_gain = held("neg_half_gain", [P, 2, PACK], F32)
-        nc.vector.tensor_scalar(neg_half_gain[:], gain_sb[:], -0.5, None, ALU.mult)
 
         v_c = {}
-        for a in range(2):
-            for h in range(2):
-                g = held("v_c%d%d" % (a, h), [P, BANK], U32)
-                nc.vector.tensor_copy(g[:], tab_w[a][:].bitcast(U32).indirect(idx[:, 32 * h : 32 * (h + 1)]))
-                v_c[a, h] = g
+        g = placed("v_c0", 53, [P, S], U32)
+        nc.vector.tensor_copy(g[:], tab_w[0][:].bitcast(U32).indirect(idx[:]))
+        for h in range(2):
+            v_c[0, h] = g[:, BANK * h : BANK * (h + 1)]
+        for h in range(2):
+            g = held("v_c1%d" % h, [P, BANK], U32)
+            nc.vector.tensor_copy(g[:], tab_w[1][:].bitcast(U32).indirect(idx[:, 32 * h : 32 * (h + 1)]))
+            v_c[1, h] = g[:]
 
+        w2_raw = {}
+
+        def w2_load(b, a, tag):
+            w2_raw[b, a] = placed("w2_raw%d%d" % (b, a), tag, [P, PACK, PASS], F32)
+            nc.sync.dma_start(
+                w2_raw[b, a][:],
+                w2[PASS * a : PASS * (a + 1), PASS * b : PASS * (b + 1)].rearrange("(p j) c -> p j c", j=PACK),
+            )
+
+        w3_raw = {}
+
+        def w3_load(b, tag):
+            w3_raw[b] = placed("w3_raw%d" % b, tag, [P, PACK, N], F32)
+            rows = w3[PASS * b : PASS * (b + 1), :].rearrange("(g t e) n -> t g e n", t=PACK, e=8)
+            for t in range(PACK):
+                nc.sync.dma_start(w3_raw[b][:, t, :], rows[t])
+
+        w2_load(0, 0, 41)
+        w2_load(0, 1, 0)
         tab2_w = []
         for a in range(2):
-            tw = shared("tab2_w%d" % a, "mid%d" % a, [P, T2], I32)
+            tw = placed("tab2_w%d" % a, 9 + 8 * a, [P, T2], I32)
             nc.sync.dma_start(tw[:], tab2_words[a].rearrange("p t i -> p (t i)").bitcast(I32))
             tab2_w.append(tw)
-        w2_raw = {}
+        gain_rows = placed("gain_rows", 8, [P, P], F32)
+        nc.gpsimd.memset(gain_rows[:], 0.0)
         for b in range(2):
-            raw = shared("w2_raw%d" % b, "big%d" % b, [P, 2 * PACK * PASS], F32)
-            for a in range(2):
-                w2_raw[b, a] = raw[:, PACK * PASS * a : PACK * PASS * (a + 1)].rearrange("p (j c) -> p j c", j=PACK)
-                nc.sync.dma_start(
-                    w2_raw[b, a],
-                    w2[PASS * a : PASS * (a + 1), PASS * b : PASS * (b + 1)].rearrange("(p j) c -> p j c", j=PACK),
-                )
+            nc.sync.dma_start(
+                gain_rows[PACK * b : PACK * (b + 1), :].rearrange("t (g e) -> t g e", e=8),
+                gain.rearrange("(b g t e) -> b t g e", b=2, t=PACK, e=8)[b],
+            )
+        ident = held("ident", [P, P], F32)
+        make_identity(nc, ident[:])
+        w2_load(1, 0, 25)
         v2_c = []
-        for a in range(2):
+
+        def v2_gather(a):
             g = held("v2_c%d" % a, [P, M], U32)
             nc.vector.tensor_copy(g[:], tab2_w[a][:].bitcast(U32).indirect(idx2[:]))
             v2_c.append(g)
-
-        w3_raw = []
-        for b in range(2):
-            raw = shared("w3_raw%d" % b, "mid%d" % b, [P, PACK, N], F32)
-            nc.sync.dma_start(raw[:], w3[PASS * b : PASS * (b + 1), :].rearrange("(p j) n -> p j n", j=PACK))
-            w3_raw.append(raw)
 
         te = {}
 
@@ -145,7 +163,7 @@ def tile_list_stemma_innovation_scores_kernel(
                     out=acc[:],
                     lhsT=w1_c[:, 2 * c0 : 2 * (c0 + P)].bitcast(FP4X4),
                     lhsT_scale=planes[a][:, S + PASS * b + P * t : S + PASS * b + P * (t + 1)],
-                    rhs=v_c[a, h][:].bitcast(FP8X4),
+                    rhs=v_c[a, h].bitcast(FP8X4),
                     rhs_scale=planes[a][:, BANK * h : BANK * (h + 1)],
                     start=(a == 0), stop=(a == 1),
                 )
@@ -155,7 +173,10 @@ def tile_list_stemma_innovation_scores_kernel(
 
         def w2_cast(b, a, copy):
             wb = ring.tile([P, PACK, P, PACK], BF16, name="w2_b", align_bytes=64)
-            copy(wb[:].rearrange("p t m j -> p m j t"), w2_raw[b, a].rearrange("p j (m t) -> p m j t", t=PACK))
+            copy(
+                wb[:].rearrange("p t (g e) j -> p t g e j", e=8),
+                w2_raw[b, a][:].rearrange("p j (g t e) -> p t g e j", t=PACK, e=8),
+            )
             w2_b[b, a] = wb
 
         def w2_quant(b, a):
@@ -179,19 +200,27 @@ def tile_list_stemma_innovation_scores_kernel(
                     rhs_scale=planes[a][:, S + H :],
                     start=(a == 0), stop=(a == 1),
                 )
-            tcs[b, t] = ring.tile([P, M], F32, name="tc")
+            tcs[b, t] = held("tc%d%d" % (b, t), [P, M], F32)
             nc.scalar.activation(tcs[b, t][:], acc[:], ACT.Tanh, scale=0.5)
 
         z_rows = {}
 
+        us = {}
+
+        def product(b, t, m0, m1, tag=None):
+            name = "u%d%d_%d" % (b, t, m0)
+            u = placed(name, 41, [P, m1 - m0], F32) if tag == "mid0" else shared(name, tag or name, [P, m1 - m0], F32)
+            nc.vector.tensor_tensor(u[:], te[b, t][:].indirect(p1[:, m0 // 16 : m1 // 16]), tcs[b, t][:, m0:m1], ALU.mult)
+            us[b, t, m0] = u
+
         def xor_rows(b, t, m0, m1):
             if (b, m0) not in z_rows:
                 z_rows[b, m0] = held("z_rows%d_%d" % (b, m0), [P, PACK, m1 - m0], BF16)
-            u = ring.tile([P, m1 - m0], F32, name="u")
-            nc.vector.tensor_tensor(u[:], te[b, t][:].indirect(p1[:, m0 // 16 : m1 // 16]), tcs[b, t][:, m0:m1], ALU.mult)
+            u = us[b, t, m0]
             nc.scalar.activation(
                 z_rows[b, m0][:, t, :], u[:], ACT.Identity,
-                scale=neg_half_gain[:, b, t : t + 1], bias=half_gain[:, b, t : t + 1],
+                scale=neg_half_gain[:, PACK * b + t : PACK * b + t + 1],
+                bias=half_gain[:, PACK * b + t : PACK * b + t + 1],
             )
 
         z_b = {}
@@ -214,8 +243,8 @@ def tile_list_stemma_innovation_scores_kernel(
         w3_c, w3_s = [], []
 
         def w3_make(b):
-            wb = held("w3_b%d" % b, [P, N, PACK], BF16)
-            nc.vector.tensor_copy(
+            wb = shared("w3_b%d" % b, "w3_b%d" % b, [P, N, PACK], BF16)
+            nc.scalar.copy(
                 wb[:].rearrange("p (c i) j -> p c j i", i=4),
                 w3_raw[b][:].rearrange("p j (c i) -> p c j i", i=4),
             )
@@ -245,27 +274,43 @@ def tile_list_stemma_innovation_scores_kernel(
         for t in range(PACK):
             for h in range(2):
                 x1_half(0, t, h)
-        for a in range(2):
-            w2_cast(0, a, nc.vector.tensor_copy)
+        w2_cast(0, 0, nc.vector.tensor_copy)
+        w2_load(1, 1, 41)
+        w2_cast(0, 1, nc.vector.tensor_copy)
+        w3_load(0, 0)
         for a in range(2):
             w2_quant(0, a)
+        for a in range(2):
+            v2_gather(a)
+        w3_load(1, 9)
         for t in range(PACK):
             b_tile(0, t)
-            xor_rows(0, t, 0, M)
         for t in range(PACK):
             for h in range(2):
                 x1_half(1, t, h)
+        w2_cast(1, 0, nc.scalar.copy)
+        w2_cast(1, 1, nc.vector.tensor_copy)
         for a in range(2):
-            w2_cast(1, a, nc.scalar.copy)
             w2_quant(1, a)
-        z_weave(0, 0, M)
-        z_quant(0, 0, M)
         for t in range(PACK):
             b_tile(1, t)
+        for t in range(PACK):
+            product(0, t, 0, M, "mid0" if t == 2 else None)
+        turned = psum.tile([P, BANK], F32, name="acc", bufs=6)
+        nc.tensor.transpose(turned[:, :P], gain_rows[:], ident[:])
+        half_gain = held("half_gain", [P, 2 * PACK], F32)
+        nc.scalar.activation(half_gain[:], turned[:, : 2 * PACK], ACT.Copy, scale=0.5)
+        neg_half_gain = held("neg_half_gain", [P, 2 * PACK], F32)
+        nc.scalar.activation(neg_half_gain[:], turned[:, : 2 * PACK], ACT.Copy, scale=-0.5)
+        for t in range(PACK):
+            xor_rows(0, t, 0, M)
+        z_weave(0, 0, M)
+        z_quant(0, 0, M)
         for b in range(2):
             w3_make(b)
         for m0, m1 in OUT_PIECES:
             for t in range(PACK):
+                product(1, t, m0, m1, "w3_b1" if (t == 0 and m0 > 0) else None)
                 xor_rows(1, t, m0, m1)
             z_weave(1, m0, m1)
             z_quant(1, m0, m1)

@@ -21,6 +21,7 @@ P = 128
 PACK = 4
 PASS = P * PACK
 BANK = 512
+EARLY_PICKS = 2
 OUT_PIECES = [(0, 256), (256, 512)]
 
 
@@ -32,7 +33,6 @@ def tile_list_stemma_innovation_scores_kernel(
     with ExitStack() as ctx:
         lists = ctx.enter_context(tc.tile_pool(name="lists", bufs=1))
         keep = ctx.enter_context(tc.tile_pool(name="keep", bufs=1))
-        ring = ctx.enter_context(tc.tile_pool(name="ring", bufs=4))
         arena = ctx.enter_context(tc.tile_pool(name="arena", bufs=1))
         psum = ctx.enter_context(tc.psum_pool(name="psum", bufs=1))
 
@@ -67,7 +67,7 @@ def tile_list_stemma_innovation_scores_kernel(
         nc.sync.dma_start(w1_s_raw[0:32, :].bitcast(I32), w1_scales.rearrange("a q c -> (a q) c").bitcast(I32))
         p1 = lists.tile([P, M // 16], U16, name="p1")
         nc.sync.dma_start(p1[:], pos1)
-        w1_raw = placed("w1_raw", 41, [P, 4 * H], U8)
+        w1_raw = held("w1_raw", [P, 4 * H], U8)
         nc.sync.dma_start(
             w1_raw[:].bitcast(I32).rearrange("p (a c) -> p a c", a=2),
             w1_words.bitcast(I32).rearrange("a p c -> p a c"),
@@ -80,7 +80,7 @@ def tile_list_stemma_innovation_scores_kernel(
 
         v_s_got = held("v_s_got", [P, S], U8)
         nc.vector.tensor_copy(v_s_got[:], tab_s[:].indirect(idx[:]))
-        v2_s_got = placed("v2_s_got", 52.75, [P, M], U8)
+        v2_s_got = placed("v2_s_got", 44.75, [P, M], U8)
         nc.vector.tensor_copy(v2_s_got[:], tab2_s[:].indirect(idx2[:]))
         nc.vector.tensor_copy(planes[0][0:32, :S].bitcast(I32), v_s_got[0:32, :].bitcast(I32))
         nc.vector.tensor_copy(
@@ -90,18 +90,17 @@ def tile_list_stemma_innovation_scores_kernel(
         nc.vector.tensor_copy(planes[0][0:32, S + H :].bitcast(I32), v2_s_got[0:32, :].bitcast(I32))
         for a in range(2):
             for q in range(1 - a, 4):
-                queue = nc.gpsimd if (a, q) == (0, 1) else nc.scalar
                 row = 16 * a + 4 * q
-                queue.dma_start(planes[a][32 * q : 32 * q + 4, :].bitcast(I32), planes[0][row : row + 4, :].bitcast(I32))
+                nc.scalar.dma_start(planes[a][32 * q : 32 * q + 4, :].bitcast(I32), planes[0][row : row + 4, :].bitcast(I32))
 
-        w1_c = placed("w1_c", 49, [P, 4 * H], U8)
+        w1_c = placed("w1_c", 41, [P, 4 * H], U8)
         nc.vector.tensor_copy(
             w1_c[:].bitcast(I32).rearrange("p (b t g e) -> p b t g e", t=PACK, g=16, e=4),
             w1_raw[:].bitcast(I32).rearrange("p (b g t e) -> p b t g e", t=PACK, g=16, e=4),
         )
 
         v_c = {}
-        g = placed("v_c0", 53, [P, S], U32)
+        g = placed("v_c0", 45, [P, S], U32)
         nc.vector.tensor_copy(g[:], tab_w[0][:].bitcast(U32).indirect(idx[:]))
         for h in range(2):
             v_c[0, h] = g[:, BANK * h : BANK * (h + 1)]
@@ -119,19 +118,19 @@ def tile_list_stemma_innovation_scores_kernel(
                 w2[PASS * a : PASS * (a + 1), PASS * b : PASS * (b + 1)].rearrange("(p j) c -> p j c", j=PACK),
             )
 
-        w3_raw = {}
+        def w3_load():
+            raw = placed("w3_raw", 9, [P, 2, PACK, N], F32)
+            rows = w3.rearrange("(b g t e) n -> b t g e n", b=2, t=PACK, e=8)
+            for b in range(2):
+                for t in range(PACK):
+                    nc.sync.dma_start(raw[:, b, t, :], rows[b, t])
+            return raw
 
-        def w3_load(b, tag):
-            w3_raw[b] = placed("w3_raw%d" % b, tag, [P, PACK, N], F32)
-            rows = w3[PASS * b : PASS * (b + 1), :].rearrange("(g t e) n -> t g e n", t=PACK, e=8)
-            for t in range(PACK):
-                nc.sync.dma_start(w3_raw[b][:, t, :], rows[t])
-
-        w2_load(0, 0, 41)
-        w2_load(0, 1, 0)
+        w2_load(0, 0, 0)
+        w2_load(0, 1, 9)
         tab2_w = []
         for a in range(2):
-            tw = placed("tab2_w%d" % a, 9 + 8 * a, [P, T2], I32)
+            tw = placed("tab2_w%d" % a, 17 + 8 * a, [P, T2], I32)
             nc.sync.dma_start(tw[:], tab2_words[a].rearrange("p t i -> p (t i)").bitcast(I32))
             tab2_w.append(tw)
         gain_rows = placed("gain_rows", 8, [P, P], F32)
@@ -143,7 +142,7 @@ def tile_list_stemma_innovation_scores_kernel(
             )
         ident = held("ident", [P, P], F32)
         make_identity(nc, ident[:])
-        w2_load(1, 0, 25)
+        w2_load(1, 0, 33)
         v2_c = []
 
         def v2_gather(a):
@@ -172,7 +171,8 @@ def tile_list_stemma_innovation_scores_kernel(
         w2_c, w2_s, w2_b = {}, {}, {}
 
         def w2_cast(b, a, copy):
-            wb = ring.tile([P, PACK, P, PACK], BF16, name="w2_b", align_bytes=64)
+            name = "w2_b%d%d" % (b, a)
+            wb = placed(name, 25 + 4 * a, [P, PACK, P, PACK], BF16) if b == 1 else held(name, [P, PACK, P, PACK], BF16)
             copy(
                 wb[:].rearrange("p t (g e) j -> p t g e j", e=8),
                 w2_raw[b, a][:].rearrange("p j (g t e) -> p t g e j", t=PACK, e=8),
@@ -180,7 +180,8 @@ def tile_list_stemma_innovation_scores_kernel(
             w2_b[b, a] = wb
 
         def w2_quant(b, a):
-            w2_c[b, a] = held("w2_c%d%d" % (b, a), [P, PASS], U32)
+            name = "w2_c%d%d" % (b, a)
+            w2_c[b, a] = placed(name, 49, [P, PASS], U32) if (b, a) == (1, 1) else held(name, [P, PASS], U32)
             w2_s[b, a] = held("w2_s%d%d" % (b, a), [P, PASS], U8)
             nc.vector.quantize_mx(
                 out=w2_c[b, a][:].bitcast(FP8X4), scales=w2_s[b, a][:],
@@ -189,47 +190,60 @@ def tile_list_stemma_innovation_scores_kernel(
 
         tcs = {}
 
-        def b_tile(b, t):
+        def b_tile(b, t, m0, m1):
             acc = psum.tile([P, M], F32, name="acc_b", bufs=2)
             for a in range(2):
                 nc.tensor.matmul_mx(
-                    out=acc[:],
+                    out=acc[:, : m1 - m0],
                     lhsT=w2_c[b, a][:, P * t : P * (t + 1)].bitcast(FP8X4),
                     lhsT_scale=w2_s[b, a][:, P * t : P * (t + 1)],
-                    rhs=v2_c[a][:].bitcast(FP8X4),
-                    rhs_scale=planes[a][:, S + H :],
+                    rhs=v2_c[a][:, m0:m1].bitcast(FP8X4),
+                    rhs_scale=planes[a][:, S + H + m0 : S + H + m1],
                     start=(a == 0), stop=(a == 1),
                 )
-            tcs[b, t] = held("tc%d%d" % (b, t), [P, M], F32)
-            nc.scalar.activation(tcs[b, t][:], acc[:], ACT.Tanh, scale=0.5)
+            tcs[b, t, m0] = held("tc%d%d_%d" % (b, t, m0), [P, m1 - m0], F32)
+            nc.scalar.activation(tcs[b, t, m0][:], acc[:, : m1 - m0], ACT.Tanh, scale=0.5)
 
         z_rows = {}
 
         us = {}
 
-        def product(b, t, m0, m1, tag=None):
+        picked = {}
+
+        def pick(b, t):
+            picked[b, t] = held("picked%d%d" % (b, t), [P, M], F32)
+            nc.vector.tensor_copy(picked[b, t][:], te[b, t][:].indirect(p1[:]))
+
+        def product(b, t, m0, m1):
             name = "u%d%d_%d" % (b, t, m0)
-            u = placed(name, 41, [P, m1 - m0], F32) if tag == "mid0" else shared(name, tag or name, [P, m1 - m0], F32)
-            nc.vector.tensor_tensor(u[:], te[b, t][:].indirect(p1[:, m0 // 16 : m1 // 16]), tcs[b, t][:, m0:m1], ALU.mult)
+            u = placed(name, (0, 2, 29, 31)[t], [P, m1 - m0], F32) if b == 0 else held(name, [P, m1 - m0], F32)
+            if (b, t) in picked:
+                left = picked[b, t][:, m0:m1]
+            else:
+                left = te[b, t][:].indirect(p1[:, m0 // 16 : m1 // 16])
+            nc.vector.tensor_tensor(u[:], left, tcs[b, t, m0][:], ALU.mult)
             us[b, t, m0] = u
 
         def xor_rows(b, t, m0, m1):
             if (b, m0) not in z_rows:
                 z_rows[b, m0] = held("z_rows%d_%d" % (b, m0), [P, PACK, m1 - m0], BF16)
             u = us[b, t, m0]
-            nc.scalar.activation(
-                z_rows[b, m0][:, t, :], u[:], ACT.Identity,
-                scale=neg_half_gain[:, PACK * b + t : PACK * b + t + 1],
-                bias=half_gain[:, PACK * b + t : PACK * b + t + 1],
-            )
+            slope = neg_half_gain[:, PACK * b + t : PACK * b + t + 1]
+            level = half_gain[:, PACK * b + t : PACK * b + t + 1]
+            if b == 0 and t >= EARLY_PICKS:
+                nc.vector.tensor_scalar(z_rows[b, m0][:, t, :], u[:], slope, level, ALU.mult, ALU.add)
+            else:
+                nc.scalar.activation(z_rows[b, m0][:, t, :], u[:], ACT.Identity, scale=slope, bias=level)
 
         z_b = {}
         z_c = [held("z_c%d" % b, [P, M], U32) for b in range(2)]
         z_s = [held("z_s%d" % b, [P, M], U8) for b in range(2)]
 
         def z_weave(b, m0, m1):
-            z_b[b, m0] = held("z_b%d_%d" % (b, m0), [P, m1 - m0, PACK], BF16)
-            nc.vector.tensor_copy(
+            name = "z_b%d_%d" % (b, m0)
+            z_b[b, m0] = placed(name, 49, [P, m1 - m0, PACK], BF16) if b == 0 else held(name, [P, m1 - m0, PACK], BF16)
+            copy = nc.scalar.copy if b == 0 else nc.vector.tensor_copy
+            copy(
                 z_b[b, m0][:].rearrange("p (c i) t -> p c t i", i=4),
                 z_rows[b, m0][:].rearrange("p t (c i) -> p c t i", i=4),
             )
@@ -240,77 +254,88 @@ def tile_list_stemma_innovation_scores_kernel(
                 in_=z_b[b, m0][:].rearrange("p m t -> p (m t)"),
             )
 
-        w3_c, w3_s = [], []
+        w3_c = held("w3_c", [P, 2 * N], U32)
+        w3_s = held("w3_s", [P, 2 * N], U8)
 
-        def w3_make(b):
-            wb = shared("w3_b%d" % b, "w3_b%d" % b, [P, N, PACK], BF16)
+        def w3_make():
+            wb = held("w3_b", [P, 2, N, PACK], BF16)
             nc.scalar.copy(
-                wb[:].rearrange("p (c i) j -> p c j i", i=4),
-                w3_raw[b][:].rearrange("p j (c i) -> p c j i", i=4),
+                wb[:].rearrange("p b (c i) j -> p b c j i", i=4),
+                w3_raw[:].rearrange("p b j (c i) -> p b c j i", i=4),
             )
-            w3_c.append(held("w3_c%d" % b, [P, N], U32))
-            w3_s.append(held("w3_s%d" % b, [P, N], U8))
             nc.vector.quantize_mx(
-                out=w3_c[b][:].bitcast(FP8X4), scales=w3_s[b][:], in_=wb[:].rearrange("p n j -> p (n j)")
+                out=w3_c[:].bitcast(FP8X4), scales=w3_s[:], in_=wb[:].rearrange("p b n j -> p (b n j)")
             )
+
+        def scores(acc, n, m0, m1):
+            for b in range(2):
+                cols = slice(N * b + P * n, N * b + P * (n + 1))
+                nc.tensor.matmul_mx(
+                    out=acc,
+                    lhsT=w3_c[:, cols].bitcast(FP8X4),
+                    lhsT_scale=w3_s[:, cols],
+                    rhs=z_c[b][:, m0:m1].bitcast(FP8X4),
+                    rhs_scale=z_s[b][:, m0:m1],
+                    start=(b == 0), stop=(b == 1),
+                )
 
         def out_piece(m0, m1):
-            for n in range(2):
+            width = m1 - m0
+            if m1 < M:
                 acc = psum.tile([P, BANK], F32, name="acc", bufs=6)
-                for b in range(2):
-                    nc.tensor.matmul_mx(
-                        out=acc[:, : m1 - m0],
-                        lhsT=w3_c[b][:, P * n : P * (n + 1)].bitcast(FP8X4),
-                        lhsT_scale=w3_s[b][:, P * n : P * (n + 1)],
-                        rhs=z_c[b][:, m0:m1].bitcast(FP8X4),
-                        rhs_scale=z_s[b][:, m0:m1],
-                        start=(b == 0), stop=(b == 1),
-                    )
-                res = ring.tile([P, m1 - m0], F32, name="res")
-                copy = nc.vector.tensor_copy if (m1, n) == (M, 1) else nc.scalar.copy
-                copy(res[:], acc[:, : m1 - m0])
-                nc.sync.dma_start(out[P * n : P * (n + 1), m0:m1], res[:])
+                for n in range(2):
+                    scores(acc[:, width * n : width * (n + 1)], n, m0, m1)
+                res = held("res%d" % m0, [P, 2, width], F32)
+                nc.scalar.copy(res[:].rearrange("p n m -> p (n m)"), acc[:, : 2 * width])
+                nc.sync.dma_start(out[:, m0:m1].rearrange("(n p) m -> p n m", p=P), res[:])
+            else:
+                for n, copy in enumerate((nc.scalar.copy, nc.vector.tensor_copy)):
+                    acc = psum.tile([P, BANK], F32, name="acc", bufs=6)
+                    scores(acc[:, :width], n, m0, m1)
+                    res = held("res%d_%d" % (m0, n), [P, width], F32)
+                    copy(res[:], acc[:, :width])
+                    nc.sync.dma_start(out[P * n : P * (n + 1), m0:m1], res[:])
 
         for t in range(PACK):
             for h in range(2):
                 x1_half(0, t, h)
         w2_cast(0, 0, nc.vector.tensor_copy)
-        w2_load(1, 1, 41)
+        w2_load(1, 1, 0)
         w2_cast(0, 1, nc.vector.tensor_copy)
-        w3_load(0, 0)
+        w3_raw = w3_load()
         for a in range(2):
             w2_quant(0, a)
         for a in range(2):
             v2_gather(a)
-        w3_load(1, 9)
+        for t in range(EARLY_PICKS):
+            pick(0, t)
         for t in range(PACK):
-            b_tile(0, t)
+            b_tile(0, t, 0, M)
         for t in range(PACK):
             for h in range(2):
                 x1_half(1, t, h)
-        w2_cast(1, 0, nc.scalar.copy)
-        w2_cast(1, 1, nc.vector.tensor_copy)
         for a in range(2):
+            w2_cast(1, a, nc.vector.tensor_copy)
             w2_quant(1, a)
+        for m0, m1 in OUT_PIECES:
+            for t in range(PACK):
+                b_tile(1, t, m0, m1)
         for t in range(PACK):
-            b_tile(1, t)
-        for t in range(PACK):
-            product(0, t, 0, M, "mid0" if t == 2 else None)
+            product(0, t, 0, M)
         turned = psum.tile([P, BANK], F32, name="acc", bufs=6)
         nc.tensor.transpose(turned[:, :P], gain_rows[:], ident[:])
         half_gain = held("half_gain", [P, 2 * PACK], F32)
-        nc.scalar.activation(half_gain[:], turned[:, : 2 * PACK], ACT.Copy, scale=0.5)
+        nc.vector.tensor_scalar(half_gain[:], turned[:, : 2 * PACK], 0.5, None, ALU.mult)
         neg_half_gain = held("neg_half_gain", [P, 2 * PACK], F32)
-        nc.scalar.activation(neg_half_gain[:], turned[:, : 2 * PACK], ACT.Copy, scale=-0.5)
+        nc.vector.tensor_scalar(neg_half_gain[:], turned[:, : 2 * PACK], -0.5, None, ALU.mult)
         for t in range(PACK):
             xor_rows(0, t, 0, M)
+        w3_make()
         z_weave(0, 0, M)
         z_quant(0, 0, M)
-        for b in range(2):
-            w3_make(b)
         for m0, m1 in OUT_PIECES:
             for t in range(PACK):
-                product(1, t, m0, m1, "w3_b1" if (t == 0 and m0 > 0) else None)
+                product(1, t, m0, m1)
                 xor_rows(1, t, m0, m1)
             z_weave(1, m0, m1)
             z_quant(1, m0, m1)

@@ -20,9 +20,27 @@ ALU = mybir.AluOpType
 P = 128
 PACK = 4
 PASS = P * PACK
+RUN = 8
 BANK = 512
-EARLY_PICKS = 2
-OUT_PIECES = [(0, 256), (256, 512)]
+LIST_ROWS = 16
+SCALE_ROWS = 32
+ACC_BANKS = 6
+
+V_AT, W1_AT, V2_AT = 0, S, S + H
+
+HALVES = [(0, M // 2), (M // 2, M)]
+
+KIB = 1024
+AT_TAB = (4 * KIB, 25 * KIB)
+AT_W2 = {(0, 0): 0, (0, 1): 9 * KIB, (1, 0): 33 * KIB, (1, 1): 0}
+AT_GAIN = 8 * KIB
+AT_TAB2 = (17 * KIB, 25 * KIB)
+AT_W3 = 9 * KIB
+AT_W1_CODES = 41 * KIB
+AT_V_CODES = 45 * KIB
+AT_V2_SCALES = AT_V_CODES - M // 2
+AT_LAST_W2_CODES = 49 * KIB
+AT_LAST_W2_ROUNDED = 53 * KIB
 
 
 def tile_list_stemma_innovation_scores_kernel(
@@ -33,310 +51,292 @@ def tile_list_stemma_innovation_scores_kernel(
     with ExitStack() as ctx:
         lists = ctx.enter_context(tc.tile_pool(name="lists", bufs=1))
         keep = ctx.enter_context(tc.tile_pool(name="keep", bufs=1))
-        arena = ctx.enter_context(tc.tile_pool(name="arena", bufs=1))
+        reused = ctx.enter_context(tc.tile_pool(name="reused", bufs=1))
         psum = ctx.enter_context(tc.psum_pool(name="psum", bufs=1))
 
-        def held(name, shape, dtype):
-            return keep.tile(shape, dtype, name=name, align_bytes=64)
+        def sbuf(name, shape, dtype, at=None):
+            if at is None:
+                return keep.tile(shape, dtype, name=name, align_bytes=64)
+            return reused.tile(shape, dtype, name=name, align_bytes=64, offset=at)
 
-        def shared(name, tag, shape, dtype):
-            return keep.tile(shape, dtype, name=name, tag=tag, align_bytes=64)
-
-        def placed(name, kib, shape, dtype):
-            return arena.tile(shape, dtype, name=name, align_bytes=64, offset=int(1024 * kib))
-
-        tab_s = held("tab_s", [P, T], U8)
-        tab2_s = held("tab2_s", [P, T2], U8)
-        w1_s_raw = held("w1_s_raw", [32, H], U8)
-        warm = held("warm", [P, 2], F32)
-        nc.gpsimd.memset(warm[:], 0.0)
+        tab_s = sbuf("tab_s", [P, T], U8)
+        tab2_s = sbuf("tab2_s", [P, T2], U8)
+        w1_s_raw = sbuf("w1_s_raw", [SCALE_ROWS, H], U8)
         for rows in (tab_s, tab2_s):
             nc.vector.memset(rows[32:64, :].bitcast(I32), 0)
             nc.vector.memset(rows[64:128, :].bitcast(I32), 0)
-        planes = [held("planes%d" % a, [P, S + H + M], U8) for a in range(2)]
+        planes = [sbuf("planes%d" % a, [P, S + H + M], U8) for a in range(2)]
         for a in range(2):
             nc.gpsimd.memset(planes[a][:].bitcast(I32), 0)
-        nc.scalar.activation(warm[:, 1:2], warm[:, 0:1], ACT.Tanh, scale=0.5)
 
-        idx = lists.tile([P, S // 16], U16, name="idx")
+        idx = lists.tile([P, S // LIST_ROWS], U16, name="idx")
         nc.sync.dma_start(idx[:], offs)
-        nc.sync.dma_start(tab_s[0:32, :].bitcast(I32), tab_scales.rearrange("a q t -> (a q) t").bitcast(I32))
-        idx2 = lists.tile([P, M // 16], U16, name="idx2")
+        nc.sync.dma_start(tab_s[:SCALE_ROWS, :].bitcast(I32), tab_scales.rearrange("a q t -> (a q) t").bitcast(I32))
+        idx2 = lists.tile([P, M // LIST_ROWS], U16, name="idx2")
         nc.sync.dma_start(idx2[:], offs2)
-        nc.sync.dma_start(tab2_s[0:32, :].bitcast(I32), tab2_scales.rearrange("a q t -> (a q) t").bitcast(I32))
-        nc.sync.dma_start(w1_s_raw[0:32, :].bitcast(I32), w1_scales.rearrange("a q c -> (a q) c").bitcast(I32))
-        p1 = lists.tile([P, M // 16], U16, name="p1")
+        nc.sync.dma_start(tab2_s[:SCALE_ROWS, :].bitcast(I32), tab2_scales.rearrange("a q t -> (a q) t").bitcast(I32))
+        nc.sync.dma_start(w1_s_raw[:].bitcast(I32), w1_scales.rearrange("a q c -> (a q) c").bitcast(I32))
+        p1 = lists.tile([P, M // LIST_ROWS], U16, name="p1")
         nc.sync.dma_start(p1[:], pos1)
-        w1_raw = held("w1_raw", [P, 4 * H], U8)
+        w1_raw = sbuf("w1_raw", [P, 4 * H], U8)
         nc.sync.dma_start(
             w1_raw[:].bitcast(I32).rearrange("p (a c) -> p a c", a=2),
             w1_words.bitcast(I32).rearrange("a p c -> p a c"),
         )
         tab_w = []
         for a in range(2):
-            tw = placed("tab_w%d" % a, (4, 25)[a], [P, T], I32)
-            nc.sync.dma_start(tw[:], tab_words[a].rearrange("p t i -> p (t i)").bitcast(I32))
-            tab_w.append(tw)
+            tab_w.append(sbuf("tab_w%d" % a, [P, T], I32, AT_TAB[a]))
+            nc.sync.dma_start(tab_w[a][:], tab_words[a].rearrange("p t i -> p (t i)").bitcast(I32))
 
-        v_s_got = held("v_s_got", [P, S], U8)
-        nc.vector.tensor_copy(v_s_got[:], tab_s[:].indirect(idx[:]))
-        v2_s_got = placed("v2_s_got", 44.75, [P, M], U8)
-        nc.vector.tensor_copy(v2_s_got[:], tab2_s[:].indirect(idx2[:]))
-        nc.vector.tensor_copy(planes[0][0:32, :S].bitcast(I32), v_s_got[0:32, :].bitcast(I32))
+        v_s = sbuf("v_s", [P, S], U8)
+        nc.vector.tensor_copy(v_s[:], tab_s[:].indirect(idx[:]))
+        v2_s = sbuf("v2_s", [P, M], U8, AT_V2_SCALES)
+        nc.vector.tensor_copy(v2_s[:], tab2_s[:].indirect(idx2[:]))
+        staged = planes[0][:SCALE_ROWS, :]
+        nc.vector.tensor_copy(staged[:, V_AT:W1_AT].bitcast(I32), v_s[:SCALE_ROWS, :].bitcast(I32))
         nc.vector.tensor_copy(
-            planes[0][0:32, S : S + H].bitcast(I32).rearrange("p (b t g e) -> p b t g e", t=PACK, g=16, e=2),
-            w1_s_raw[:].bitcast(I32).rearrange("p (b g t e) -> p b t g e", t=PACK, g=16, e=2),
+            staged[:, W1_AT:V2_AT].bitcast(I32).rearrange("p (c t g e) -> p c t g e", t=PACK, g=16, e=2),
+            w1_s_raw[:].bitcast(I32).rearrange("p (c g t e) -> p c t g e", t=PACK, g=16, e=2),
         )
-        nc.vector.tensor_copy(planes[0][0:32, S + H :].bitcast(I32), v2_s_got[0:32, :].bitcast(I32))
+        nc.vector.tensor_copy(staged[:, V2_AT:].bitcast(I32), v2_s[:SCALE_ROWS, :].bitcast(I32))
         for a in range(2):
-            for q in range(1 - a, 4):
-                row = 16 * a + 4 * q
-                nc.scalar.dma_start(planes[a][32 * q : 32 * q + 4, :].bitcast(I32), planes[0][row : row + 4, :].bitcast(I32))
+            for u in range(1 - a, 4):
+                queue = nc.gpsimd if (a, u) == (0, 1) else nc.scalar
+                row = 16 * a + 4 * u
+                queue.dma_start(planes[a][32 * u : 32 * u + 4, :].bitcast(I32), staged[row : row + 4, :].bitcast(I32))
 
-        w1_c = placed("w1_c", 41, [P, 4 * H], U8)
+        w1_c = sbuf("w1_c", [P, 4 * H], U8, AT_W1_CODES)
         nc.vector.tensor_copy(
-            w1_c[:].bitcast(I32).rearrange("p (b t g e) -> p b t g e", t=PACK, g=16, e=4),
-            w1_raw[:].bitcast(I32).rearrange("p (b g t e) -> p b t g e", t=PACK, g=16, e=4),
+            w1_c[:].bitcast(I32).rearrange("p (c t g e) -> p c t g e", t=PACK, g=16, e=4),
+            w1_raw[:].bitcast(I32).rearrange("p (c g t e) -> p c t g e", t=PACK, g=16, e=4),
         )
 
+        v_c0 = sbuf("v_c0", [P, S], U32, AT_V_CODES)
+        nc.vector.tensor_copy(v_c0[:], tab_w[0][:].bitcast(U32).indirect(idx[:]))
         v_c = {}
-        g = placed("v_c0", 45, [P, S], U32)
-        nc.vector.tensor_copy(g[:], tab_w[0][:].bitcast(U32).indirect(idx[:]))
         for h in range(2):
-            v_c[0, h] = g[:, BANK * h : BANK * (h + 1)]
+            v_c[0, h] = v_c0[:, BANK * h : BANK * (h + 1)]
         for h in range(2):
-            g = held("v_c1%d" % h, [P, BANK], U32)
-            nc.vector.tensor_copy(g[:], tab_w[1][:].bitcast(U32).indirect(idx[:, 32 * h : 32 * (h + 1)]))
-            v_c[1, h] = g[:]
+            half = sbuf("v_c1%d" % h, [P, BANK], U32)
+            entries = idx[:, BANK * h // LIST_ROWS : BANK * (h + 1) // LIST_ROWS]
+            nc.vector.tensor_copy(half[:], tab_w[1][:].bitcast(U32).indirect(entries))
+            v_c[1, h] = half[:]
 
         w2_raw = {}
 
-        def w2_load(b, a, tag):
-            w2_raw[b, a] = placed("w2_raw%d%d" % (b, a), tag, [P, PACK, PASS], F32)
+        def w2_load(c, a):
+            w2_raw[c, a] = sbuf("w2_raw%d%d" % (c, a), [P, PACK, PASS], F32, AT_W2[c, a])
             nc.sync.dma_start(
-                w2_raw[b, a][:],
-                w2[PASS * a : PASS * (a + 1), PASS * b : PASS * (b + 1)].rearrange("(p j) c -> p j c", j=PACK),
+                w2_raw[c, a][:],
+                w2[PASS * a : PASS * (a + 1), PASS * c : PASS * (c + 1)].rearrange("(p i) r -> p i r", i=PACK),
             )
 
-        def w3_load():
-            raw = placed("w3_raw", 9, [P, 2, PACK, N], F32)
-            rows = w3.rearrange("(b g t e) n -> b t g e n", b=2, t=PACK, e=8)
-            for b in range(2):
-                for t in range(PACK):
-                    nc.sync.dma_start(raw[:, b, t, :], rows[b, t])
-            return raw
-
-        w2_load(0, 0, 0)
-        w2_load(0, 1, 9)
+        w2_load(0, 0)
+        w2_load(0, 1)
         tab2_w = []
         for a in range(2):
-            tw = placed("tab2_w%d" % a, 17 + 8 * a, [P, T2], I32)
-            nc.sync.dma_start(tw[:], tab2_words[a].rearrange("p t i -> p (t i)").bitcast(I32))
-            tab2_w.append(tw)
-        gain_rows = placed("gain_rows", 8, [P, P], F32)
+            tab2_w.append(sbuf("tab2_w%d" % a, [P, T2], I32, AT_TAB2[a]))
+            nc.sync.dma_start(tab2_w[a][:], tab2_words[a].rearrange("p t i -> p (t i)").bitcast(I32))
+        gain_rows = sbuf("gain_rows", [P, P], F32, AT_GAIN)
         nc.gpsimd.memset(gain_rows[:], 0.0)
-        for b in range(2):
+        for c in range(2):
             nc.sync.dma_start(
-                gain_rows[PACK * b : PACK * (b + 1), :].rearrange("t (g e) -> t g e", e=8),
-                gain.rearrange("(b g t e) -> b t g e", b=2, t=PACK, e=8)[b],
+                gain_rows[PACK * c : PACK * (c + 1), :].rearrange("t (g e) -> t g e", e=RUN),
+                gain.rearrange("(c g t e) -> c t g e", c=2, t=PACK, e=RUN)[c],
             )
-        ident = held("ident", [P, P], F32)
+        ident = sbuf("ident", [P, P], F32)
         make_identity(nc, ident[:])
-        w2_load(1, 0, 33)
+        w2_load(1, 0)
+
+        tanh_x1 = {}
+
+        def x1_tile(c, t):
+            tanh_x1[c, t] = sbuf("tanh_x1_%d%d" % (c, t), [P, S], F32)
+            col = PASS * c + P * t
+            for h in range(2):
+                acc = psum.tile([P, BANK], F32, name="acc", bufs=ACC_BANKS)
+                for a in range(2):
+                    nc.tensor.matmul_mx(
+                        out=acc[:],
+                        lhsT=w1_c[:, 2 * (H * a + col) : 2 * (H * a + col + P)].bitcast(FP4X4),
+                        lhsT_scale=planes[a][:, W1_AT + col : W1_AT + col + P],
+                        rhs=v_c[a, h].bitcast(FP8X4),
+                        rhs_scale=planes[a][:, V_AT + BANK * h : V_AT + BANK * (h + 1)],
+                        start=(a == 0), stop=(a == 1),
+                    )
+                nc.scalar.activation(tanh_x1[c, t][:, BANK * h : BANK * (h + 1)], acc[:], ACT.Tanh, scale=0.5)
+
+        w2_rounded, w2_c, w2_s = {}, {}, {}
+
+        def w2_round(c, a, at=None):
+            w2_rounded[c, a] = sbuf("w2_rounded%d%d" % (c, a), [P, PACK, P, PACK], BF16, at)
+            nc.vector.tensor_copy(
+                w2_rounded[c, a][:].rearrange("p t (g e) i -> p t g e i", e=RUN),
+                w2_raw[c, a][:].rearrange("p i (g t e) -> p t g e i", t=PACK, e=RUN),
+            )
+
+        def w2_quantise(c, a, at=None):
+            w2_c[c, a] = sbuf("w2_c%d%d" % (c, a), [P, PASS], U32, at)
+            w2_s[c, a] = sbuf("w2_s%d%d" % (c, a), [P, PASS], U8)
+            nc.vector.quantize_mx(
+                out=w2_c[c, a][:].bitcast(FP8X4), scales=w2_s[c, a][:],
+                in_=w2_rounded[c, a][:].rearrange("p t m i -> p (t m i)"),
+            )
+
         v2_c = []
 
         def v2_gather(a):
-            g = held("v2_c%d" % a, [P, M], U32)
-            nc.vector.tensor_copy(g[:], tab2_w[a][:].bitcast(U32).indirect(idx2[:]))
-            v2_c.append(g)
+            v2_c.append(sbuf("v2_c%d" % a, [P, M], U32))
+            nc.vector.tensor_copy(v2_c[a][:], tab2_w[a][:].bitcast(U32).indirect(idx2[:]))
 
-        te = {}
+        tanh_b = {}
 
-        def x1_half(b, t, h):
-            if (b, t) not in te:
-                te[b, t] = held("te%d%d" % (b, t), [P, S], F32)
-            acc = psum.tile([P, BANK], F32, name="acc", bufs=6)
-            for a in range(2):
-                c0 = H * a + PASS * b + P * t
-                nc.tensor.matmul_mx(
-                    out=acc[:],
-                    lhsT=w1_c[:, 2 * c0 : 2 * (c0 + P)].bitcast(FP4X4),
-                    lhsT_scale=planes[a][:, S + PASS * b + P * t : S + PASS * b + P * (t + 1)],
-                    rhs=v_c[a, h].bitcast(FP8X4),
-                    rhs_scale=planes[a][:, BANK * h : BANK * (h + 1)],
-                    start=(a == 0), stop=(a == 1),
-                )
-            nc.scalar.activation(te[b, t][:, BANK * h : BANK * (h + 1)], acc[:], ACT.Tanh, scale=0.5)
-
-        w2_c, w2_s, w2_b = {}, {}, {}
-
-        def w2_cast(b, a, copy):
-            name = "w2_b%d%d" % (b, a)
-            wb = placed(name, 25 + 4 * a, [P, PACK, P, PACK], BF16) if b == 1 else held(name, [P, PACK, P, PACK], BF16)
-            copy(
-                wb[:].rearrange("p t (g e) j -> p t g e j", e=8),
-                w2_raw[b, a][:].rearrange("p j (g t e) -> p t g e j", t=PACK, e=8),
-            )
-            w2_b[b, a] = wb
-
-        def w2_quant(b, a):
-            name = "w2_c%d%d" % (b, a)
-            w2_c[b, a] = placed(name, 49, [P, PASS], U32) if (b, a) == (1, 1) else held(name, [P, PASS], U32)
-            w2_s[b, a] = held("w2_s%d%d" % (b, a), [P, PASS], U8)
-            nc.vector.quantize_mx(
-                out=w2_c[b, a][:].bitcast(FP8X4), scales=w2_s[b, a][:],
-                in_=w2_b[b, a][:].rearrange("p t m j -> p (t m j)"),
-            )
-
-        tcs = {}
-
-        def b_tile(b, t, m0, m1):
+        def b_tile(c, t, m0, m1):
             acc = psum.tile([P, M], F32, name="acc_b", bufs=2)
             for a in range(2):
                 nc.tensor.matmul_mx(
                     out=acc[:, : m1 - m0],
-                    lhsT=w2_c[b, a][:, P * t : P * (t + 1)].bitcast(FP8X4),
-                    lhsT_scale=w2_s[b, a][:, P * t : P * (t + 1)],
+                    lhsT=w2_c[c, a][:, P * t : P * (t + 1)].bitcast(FP8X4),
+                    lhsT_scale=w2_s[c, a][:, P * t : P * (t + 1)],
                     rhs=v2_c[a][:, m0:m1].bitcast(FP8X4),
-                    rhs_scale=planes[a][:, S + H + m0 : S + H + m1],
+                    rhs_scale=planes[a][:, V2_AT + m0 : V2_AT + m1],
                     start=(a == 0), stop=(a == 1),
                 )
-            tcs[b, t, m0] = held("tc%d%d_%d" % (b, t, m0), [P, m1 - m0], F32)
-            nc.scalar.activation(tcs[b, t, m0][:], acc[:, : m1 - m0], ACT.Tanh, scale=0.5)
-
-        z_rows = {}
-
-        us = {}
+            tanh_b[c, t, m0] = sbuf("tanh_b%d%d_%d" % (c, t, m0), [P, m1 - m0], F32)
+            nc.scalar.activation(tanh_b[c, t, m0][:], acc[:, : m1 - m0], ACT.Tanh, scale=0.5)
 
         picked = {}
 
-        def pick(b, t):
-            picked[b, t] = held("picked%d%d" % (b, t), [P, M], F32)
-            nc.vector.tensor_copy(picked[b, t][:], te[b, t][:].indirect(p1[:]))
+        def pick(t, at=None):
+            picked[t] = sbuf("picked%d" % t, [P, M], F32, at)
+            nc.vector.tensor_copy(picked[t][:], tanh_x1[0, t][:].indirect(p1[:]))
 
-        def product(b, t, m0, m1):
-            name = "u%d%d_%d" % (b, t, m0)
-            u = placed(name, (0, 2, 29, 31)[t], [P, m1 - m0], F32) if b == 0 else held(name, [P, m1 - m0], F32)
-            if (b, t) in picked:
-                left = picked[b, t][:, m0:m1]
+        products = {}
+
+        def product(c, t, m0, m1, at=None):
+            products[c, t, m0] = sbuf("product%d%d_%d" % (c, t, m0), [P, m1 - m0], F32, at)
+            if c == 0 and t in picked:
+                exemplar = picked[t][:, m0:m1]
             else:
-                left = te[b, t][:].indirect(p1[:, m0 // 16 : m1 // 16])
-            nc.vector.tensor_tensor(u[:], left, tcs[b, t, m0][:], ALU.mult)
-            us[b, t, m0] = u
+                exemplar = tanh_x1[c, t][:].indirect(p1[:, m0 // LIST_ROWS : m1 // LIST_ROWS])
+            nc.vector.tensor_tensor(products[c, t, m0][:], exemplar, tanh_b[c, t, m0][:], ALU.mult)
 
-        def xor_rows(b, t, m0, m1):
-            if (b, m0) not in z_rows:
-                z_rows[b, m0] = held("z_rows%d_%d" % (b, m0), [P, PACK, m1 - m0], BF16)
-            u = us[b, t, m0]
-            slope = neg_half_gain[:, PACK * b + t : PACK * b + t + 1]
-            level = half_gain[:, PACK * b + t : PACK * b + t + 1]
-            if b == 0 and t >= EARLY_PICKS:
-                nc.vector.tensor_scalar(z_rows[b, m0][:, t, :], u[:], slope, level, ALU.mult, ALU.add)
+        z_rows = {}
+
+        def z_row(c, t, m0, m1, on_vector=False):
+            if (c, m0) not in z_rows:
+                z_rows[c, m0] = sbuf("z_rows%d_%d" % (c, m0), [P, PACK, m1 - m0], BF16)
+            slope = minus_half_gain[:, PACK * c + t : PACK * c + t + 1]
+            level = half_gain[:, PACK * c + t : PACK * c + t + 1]
+            if on_vector:
+                nc.vector.tensor_scalar(z_rows[c, m0][:, t, :], products[c, t, m0][:], slope, level, ALU.mult, ALU.add)
             else:
-                nc.scalar.activation(z_rows[b, m0][:, t, :], u[:], ACT.Identity, scale=slope, bias=level)
+                nc.scalar.activation(
+                    z_rows[c, m0][:, t, :], products[c, t, m0][:], ACT.Identity, scale=slope, bias=level
+                )
 
-        z_b = {}
-        z_c = [held("z_c%d" % b, [P, M], U32) for b in range(2)]
-        z_s = [held("z_s%d" % b, [P, M], U8) for b in range(2)]
+        z_c = [sbuf("z_c%d" % c, [P, M], U32) for c in range(2)]
+        z_s = [sbuf("z_s%d" % c, [P, M], U8) for c in range(2)]
 
-        def z_weave(b, m0, m1):
-            name = "z_b%d_%d" % (b, m0)
-            z_b[b, m0] = placed(name, 49, [P, m1 - m0, PACK], BF16) if b == 0 else held(name, [P, m1 - m0, PACK], BF16)
-            copy = nc.scalar.copy if b == 0 else nc.vector.tensor_copy
+        def z_quantise(c, m0, m1, copy, at=None):
+            woven = sbuf("z_woven%d_%d" % (c, m0), [P, m1 - m0, PACK], BF16, at)
             copy(
-                z_b[b, m0][:].rearrange("p (c i) t -> p c t i", i=4),
-                z_rows[b, m0][:].rearrange("p t (c i) -> p c t i", i=4),
-            )
-
-        def z_quant(b, m0, m1):
-            nc.vector.quantize_mx(
-                out=z_c[b][:, m0:m1].bitcast(FP8X4), scales=z_s[b][:, m0:m1],
-                in_=z_b[b, m0][:].rearrange("p m t -> p (m t)"),
-            )
-
-        w3_c = held("w3_c", [P, 2 * N], U32)
-        w3_s = held("w3_s", [P, 2 * N], U8)
-
-        def w3_make():
-            wb = held("w3_b", [P, 2, N, PACK], BF16)
-            nc.scalar.copy(
-                wb[:].rearrange("p b (c i) j -> p b c j i", i=4),
-                w3_raw[:].rearrange("p b j (c i) -> p b c j i", i=4),
+                woven[:].rearrange("p (f i) t -> p f t i", i=4),
+                z_rows[c, m0][:].rearrange("p t (f i) -> p f t i", i=4),
             )
             nc.vector.quantize_mx(
-                out=w3_c[:].bitcast(FP8X4), scales=w3_s[:], in_=wb[:].rearrange("p b n j -> p (b n j)")
+                out=z_c[c][:, m0:m1].bitcast(FP8X4), scales=z_s[c][:, m0:m1],
+                in_=woven[:].rearrange("p m t -> p (m t)"),
             )
+
+        w3_c = sbuf("w3_c", [P, 2 * N], U32)
+        w3_s = sbuf("w3_s", [P, 2 * N], U8)
 
         def scores(acc, n, m0, m1):
-            for b in range(2):
-                cols = slice(N * b + P * n, N * b + P * (n + 1))
+            for c in range(2):
+                cols = slice(N * c + P * n, N * c + P * (n + 1))
                 nc.tensor.matmul_mx(
                     out=acc,
                     lhsT=w3_c[:, cols].bitcast(FP8X4),
                     lhsT_scale=w3_s[:, cols],
-                    rhs=z_c[b][:, m0:m1].bitcast(FP8X4),
-                    rhs_scale=z_s[b][:, m0:m1],
-                    start=(b == 0), stop=(b == 1),
+                    rhs=z_c[c][:, m0:m1].bitcast(FP8X4),
+                    rhs_scale=z_s[c][:, m0:m1],
+                    start=(c == 0), stop=(c == 1),
                 )
 
-        def out_piece(m0, m1):
-            width = m1 - m0
-            if m1 < M:
-                acc = psum.tile([P, BANK], F32, name="acc", bufs=6)
-                for n in range(2):
-                    scores(acc[:, width * n : width * (n + 1)], n, m0, m1)
-                res = held("res%d" % m0, [P, 2, width], F32)
-                nc.scalar.copy(res[:].rearrange("p n m -> p (n m)"), acc[:, : 2 * width])
-                nc.sync.dma_start(out[:, m0:m1].rearrange("(n p) m -> p n m", p=P), res[:])
-            else:
-                for n, copy in enumerate((nc.scalar.copy, nc.vector.tensor_copy)):
-                    acc = psum.tile([P, BANK], F32, name="acc", bufs=6)
-                    scores(acc[:, :width], n, m0, m1)
-                    res = held("res%d_%d" % (m0, n), [P, width], F32)
-                    copy(res[:], acc[:, :width])
-                    nc.sync.dma_start(out[P * n : P * (n + 1), m0:m1], res[:])
-
+        last = PACK - 1
         for t in range(PACK):
-            for h in range(2):
-                x1_half(0, t, h)
-        w2_cast(0, 0, nc.vector.tensor_copy)
-        w2_load(1, 1, 0)
-        w2_cast(0, 1, nc.vector.tensor_copy)
-        w3_raw = w3_load()
+            x1_tile(0, t)
+        w2_round(0, 0)
+        w2_load(1, 1)
+        w2_round(0, 1)
+        w3_raw = sbuf("w3_raw", [P, 2, PACK, N], F32, AT_W3)
+        w3_rows = w3.rearrange("(c g t e) n -> c t g e n", c=2, t=PACK, e=RUN)
+        for c in range(2):
+            for t in range(PACK):
+                nc.sync.dma_start(w3_raw[:, c, t, :], w3_rows[c, t])
         for a in range(2):
-            w2_quant(0, a)
+            w2_quantise(0, a)
         for a in range(2):
             v2_gather(a)
-        for t in range(EARLY_PICKS):
-            pick(0, t)
+        pick(0)
+        pick(1)
+        pick(2, AT_TAB2[1] + 4 * KIB)
         for t in range(PACK):
             b_tile(0, t, 0, M)
+
         for t in range(PACK):
-            for h in range(2):
-                x1_half(1, t, h)
-        for a in range(2):
-            w2_cast(1, a, nc.vector.tensor_copy)
-            w2_quant(1, a)
-        for m0, m1 in OUT_PIECES:
+            x1_tile(1, t)
+        w2_round(1, 0, AT_TAB2[1])
+        w2_quantise(1, 0)
+        w2_round(1, 1, AT_LAST_W2_ROUNDED)
+        w2_quantise(1, 1, AT_LAST_W2_CODES)
+        for m0, m1 in HALVES:
             for t in range(PACK):
                 b_tile(1, t, m0, m1)
-        for t in range(PACK):
-            product(0, t, 0, M)
-        turned = psum.tile([P, BANK], F32, name="acc", bufs=6)
+
+        for t in range(last):
+            product(0, t, 0, M, AT_W2[1, 1] + 2 * KIB * t)
+        product(0, last, 0, M, AT_LAST_W2_ROUNDED)
+        turned = psum.tile([P, BANK], F32, name="acc", bufs=ACC_BANKS)
         nc.tensor.transpose(turned[:, :P], gain_rows[:], ident[:])
-        half_gain = held("half_gain", [P, 2 * PACK], F32)
+        half_gain = sbuf("half_gain", [P, 2 * PACK], F32)
         nc.vector.tensor_scalar(half_gain[:], turned[:, : 2 * PACK], 0.5, None, ALU.mult)
-        neg_half_gain = held("neg_half_gain", [P, 2 * PACK], F32)
-        nc.vector.tensor_scalar(neg_half_gain[:], turned[:, : 2 * PACK], -0.5, None, ALU.mult)
+        minus_half_gain = sbuf("minus_half_gain", [P, 2 * PACK], F32)
+        nc.vector.tensor_scalar(minus_half_gain[:], turned[:, : 2 * PACK], -0.5, None, ALU.mult)
         for t in range(PACK):
-            xor_rows(0, t, 0, M)
-        w3_make()
-        z_weave(0, 0, M)
-        z_quant(0, 0, M)
-        for m0, m1 in OUT_PIECES:
+            z_row(0, t, 0, M, on_vector=(t == last))
+
+        w3_rounded = sbuf("w3_rounded", [P, 2, N, PACK], BF16)
+        nc.scalar.copy(
+            w3_rounded[:].rearrange("p c (f i) t -> p c f t i", i=4),
+            w3_raw[:].rearrange("p c t (f i) -> p c f t i", i=4),
+        )
+        nc.vector.quantize_mx(
+            out=w3_c[:].bitcast(FP8X4), scales=w3_s[:], in_=w3_rounded[:].rearrange("p c n t -> p (c n t)")
+        )
+        z_quantise(0, 0, M, nc.scalar.copy, AT_LAST_W2_CODES)
+
+        def z_half(m0, m1):
             for t in range(PACK):
                 product(1, t, m0, m1)
-                xor_rows(1, t, m0, m1)
-            z_weave(1, m0, m1)
-            z_quant(1, m0, m1)
-            out_piece(m0, m1)
+                z_row(1, t, m0, m1)
+            z_quantise(1, m0, m1, nc.vector.tensor_copy)
+
+        m0, m1 = HALVES[0]
+        z_half(m0, m1)
+        acc = psum.tile([P, BANK], F32, name="acc", bufs=ACC_BANKS)
+        for n in range(2):
+            scores(acc[:, (m1 - m0) * n : (m1 - m0) * (n + 1)], n, m0, m1)
+        first = sbuf("first", [P, 2, m1 - m0], F32)
+        nc.scalar.copy(first[:].rearrange("p n m -> p (n m)"), acc[:])
+        nc.sync.dma_start(out[:, m0:m1].rearrange("(n p) m -> p n m", p=P), first[:])
+
+        m0, m1 = HALVES[1]
+        z_half(m0, m1)
+        for n, copy in enumerate((nc.scalar.copy, nc.vector.tensor_copy)):
+            acc = psum.tile([P, BANK], F32, name="acc", bufs=ACC_BANKS)
+            scores(acc[:, : m1 - m0], n, m0, m1)
+            second = sbuf("second%d" % n, [P, m1 - m0], F32)
+            copy(second[:], acc[:, : m1 - m0])
+            nc.sync.dma_start(out[P * n : P * (n + 1), m0:m1], second[:])

@@ -32,7 +32,7 @@ HALVES = [(0, M // 2), (M // 2, M)]
 
 KIB = 1024
 AT_TAB = (4 * KIB, 25 * KIB)
-AT_W2 = {(0, 0): 0, (0, 1): 9 * KIB, (1, 0): 33 * KIB, (1, 1): 0}
+AT_W2 = {(0, 0): 0, (0, 1): 9 * KIB, (1, 0): 33 * KIB, (1, 1): 0 * KIB}
 AT_GAIN = 8 * KIB
 AT_TAB2 = (17 * KIB, 25 * KIB)
 AT_W3 = 9 * KIB
@@ -133,10 +133,22 @@ def tile_list_stemma_innovation_scores_kernel(
 
         w2_load(0, 0)
         w2_load(0, 1)
-        tab2_w = []
-        for a in range(2):
-            tab2_w.append(sbuf("tab2_w%d" % a, [P, T2], I32, AT_TAB2[a]))
+        tab2_w = {}
+
+        def tab2_load(a):
+            tab2_w[a] = sbuf("tab2_w%d" % a, [P, T2], I32, AT_TAB2[a])
             nc.sync.dma_start(tab2_w[a][:], tab2_words[a].rearrange("p t i -> p (t i)").bitcast(I32))
+
+        def w3_load():
+            raw = sbuf("w3_raw", [P, 2, PACK, N], F32, AT_W3)
+            w3_rows = w3.rearrange("(c g t e) n -> c t g e n", c=2, t=PACK, e=RUN)
+            for c in range(2):
+                for t in range(PACK):
+                    nc.sync.dma_start(raw[:, c, t, :], w3_rows[c, t])
+            return raw
+
+        tab2_load(0)
+        tab2_load(1)
         gain_rows = sbuf("gain_rows", [P, P], F32, AT_GAIN)
         nc.gpsimd.memset(gain_rows[:], 0.0)
         for c in range(2):
@@ -150,10 +162,11 @@ def tile_list_stemma_innovation_scores_kernel(
 
         tanh_x1 = {}
 
-        def x1_tile(c, t):
-            tanh_x1[c, t] = sbuf("tanh_x1_%d%d" % (c, t), [P, S], F32)
+        def x1_bank(c, t, h):
+            if h == 0:
+                tanh_x1[c, t] = sbuf("tanh_x1_%d%d" % (c, t), [P, S], F32)
             col = PASS * c + P * t
-            for h in range(2):
+            if True:
                 acc = psum.tile([P, BANK], F32, name="acc", bufs=ACC_BANKS)
                 for a in range(2):
                     nc.tensor.matmul_mx(
@@ -168,9 +181,9 @@ def tile_list_stemma_innovation_scores_kernel(
 
         w2_rounded, w2_c, w2_s = {}, {}, {}
 
-        def w2_round(c, a, at=None):
+        def w2_round(c, a, at=None, copy=nc.vector.tensor_copy):
             w2_rounded[c, a] = sbuf("w2_rounded%d%d" % (c, a), [P, PACK, P, PACK], BF16, at)
-            nc.vector.tensor_copy(
+            copy(
                 w2_rounded[c, a][:].rearrange("p t (g e) i -> p t g e i", e=RUN),
                 w2_raw[c, a][:].rearrange("p i (g t e) -> p t g e i", t=PACK, e=RUN),
             )
@@ -192,7 +205,7 @@ def tile_list_stemma_innovation_scores_kernel(
         tanh_b = {}
 
         def b_tile(c, t, m0, m1):
-            acc = psum.tile([P, M], F32, name="acc_b", bufs=2)
+            acc = psum.tile([P, BANK], F32, name="acc", bufs=ACC_BANKS)
             for a in range(2):
                 nc.tensor.matmul_mx(
                     out=acc[:, : m1 - m0],
@@ -203,7 +216,7 @@ def tile_list_stemma_innovation_scores_kernel(
                     start=(a == 0), stop=(a == 1),
                 )
             tanh_b[c, t, m0] = sbuf("tanh_b%d%d_%d" % (c, t, m0), [P, m1 - m0], F32)
-            nc.scalar.activation(tanh_b[c, t, m0][:], acc[:, : m1 - m0], ACT.Tanh, scale=0.5)
+            nc.scalar.activation(tanh_b[c, t, m0][:], acc[:, : m1 - m0], ACT.Tanh, scale=-0.5)
 
         picked = {}
 
@@ -219,31 +232,37 @@ def tile_list_stemma_innovation_scores_kernel(
                 exemplar = picked[t][:, m0:m1]
             else:
                 exemplar = tanh_x1[c, t][:].indirect(p1[:, m0 // LIST_ROWS : m1 // LIST_ROWS])
-            nc.vector.tensor_tensor(products[c, t, m0][:], exemplar, tanh_b[c, t, m0][:], ALU.mult)
+            nc.vector.tensor_tensor(products[c, t, m0][:], exemplar, tanh_b[c, t, 0][:, m0:m1], ALU.mult)
 
         z_rows = {}
 
         def z_row(c, t, m0, m1, on_vector=False):
-            if (c, m0) not in z_rows:
-                z_rows[c, m0] = sbuf("z_rows%d_%d" % (c, m0), [P, PACK, m1 - m0], BF16)
-            slope = minus_half_gain[:, PACK * c + t : PACK * c + t + 1]
+            if c not in z_rows:
+                z_rows[c] = sbuf("z_rows%d" % c, [P, PACK, M], BF16)
             level = half_gain[:, PACK * c + t : PACK * c + t + 1]
+            slope = level
             if on_vector:
-                nc.vector.tensor_scalar(z_rows[c, m0][:, t, :], products[c, t, m0][:], slope, level, ALU.mult, ALU.add)
+                nc.vector.tensor_scalar(z_rows[c][:, t, m0:m1], products[c, t, m0][:], slope, level, ALU.mult, ALU.add)
             else:
                 nc.scalar.activation(
-                    z_rows[c, m0][:, t, :], products[c, t, m0][:], ACT.Identity, scale=slope, bias=level
+                    z_rows[c][:, t, m0:m1], products[c, t, m0][:], ACT.Identity, scale=slope, bias=level
                 )
 
         z_c = [sbuf("z_c%d" % c, [P, M], U32) for c in range(2)]
         z_s = [sbuf("z_s%d" % c, [P, M], U8) for c in range(2)]
 
-        def z_quantise(c, m0, m1, copy, at=None):
+        woven_of = {}
+
+        def z_weave(c, m0, m1, copy, at=None):
             woven = sbuf("z_woven%d_%d" % (c, m0), [P, m1 - m0, PACK], BF16, at)
             copy(
                 woven[:].rearrange("p (f i) t -> p f t i", i=4),
-                z_rows[c, m0][:].rearrange("p t (f i) -> p f t i", i=4),
+                z_rows[c][:, :, m0:m1].rearrange("p t (f i) -> p f t i", i=4),
             )
+            woven_of[c, m0] = woven
+
+        def z_quantise(c, m0, m1):
+            woven = woven_of[c, m0]
             nc.vector.quantize_mx(
                 out=z_c[c][:, m0:m1].bitcast(FP8X4), scales=z_s[c][:, m0:m1],
                 in_=woven[:].rearrange("p m t -> p (m t)"),
@@ -252,8 +271,8 @@ def tile_list_stemma_innovation_scores_kernel(
         w3_c = sbuf("w3_c", [P, 2 * N], U32)
         w3_s = sbuf("w3_s", [P, 2 * N], U8)
 
-        def scores(acc, n, m0, m1):
-            for c in range(2):
+        def scores(acc, n, m0, m1, passes=(0, 1)):
+            for c in passes:
                 cols = slice(N * c + P * n, N * c + P * (n + 1))
                 nc.tensor.matmul_mx(
                     out=acc,
@@ -265,78 +284,72 @@ def tile_list_stemma_innovation_scores_kernel(
                 )
 
         last = PACK - 1
-        for t in range(PACK):
-            x1_tile(0, t)
+        for t0 in (0, 2):
+            for h in range(2):
+                for t in (t0, t0 + 1):
+                    x1_bank(0, t, h)
         w2_round(0, 0)
         w2_load(1, 1)
         w2_round(0, 1)
-        w3_raw = sbuf("w3_raw", [P, 2, PACK, N], F32, AT_W3)
-        w3_rows = w3.rearrange("(c g t e) n -> c t g e n", c=2, t=PACK, e=RUN)
-        for c in range(2):
-            for t in range(PACK):
-                nc.sync.dma_start(w3_raw[:, c, t, :], w3_rows[c, t])
-        for a in range(2):
-            w2_quantise(0, a)
-        for a in range(2):
-            v2_gather(a)
+        w3_raw = w3_load()
+        w2_quantise(0, 0)
+        w2_quantise(0, 1)
+        v2_gather(0)
+        v2_gather(1)
         pick(0)
         pick(1)
-        pick(2, AT_TAB2[1] + 4 * KIB)
+        for t in range(PACK):
+            for h in range(2):
+                x1_bank(1, t, h)
         for t in range(PACK):
             b_tile(0, t, 0, M)
-
-        for t in range(PACK):
-            x1_tile(1, t)
-        w2_round(1, 0, AT_TAB2[1])
-        w2_quantise(1, 0)
-        w2_round(1, 1, AT_LAST_W2_ROUNDED)
-        w2_quantise(1, 1, AT_LAST_W2_CODES)
-        for m0, m1 in HALVES:
-            for t in range(PACK):
-                b_tile(1, t, m0, m1)
-
-        for t in range(last):
-            product(0, t, 0, M, AT_W2[1, 1] + 2 * KIB * t)
-        product(0, last, 0, M, AT_LAST_W2_ROUNDED)
-        turned = psum.tile([P, BANK], F32, name="acc", bufs=ACC_BANKS)
+        turned = psum.tile([P, BANK], F32, name="late", bufs=2)
         nc.tensor.transpose(turned[:, :P], gain_rows[:], ident[:])
         half_gain = sbuf("half_gain", [P, 2 * PACK], F32)
         nc.vector.tensor_scalar(half_gain[:], turned[:, : 2 * PACK], 0.5, None, ALU.mult)
-        minus_half_gain = sbuf("minus_half_gain", [P, 2 * PACK], F32)
-        nc.vector.tensor_scalar(minus_half_gain[:], turned[:, : 2 * PACK], -0.5, None, ALU.mult)
+        w2_round(1, 0)
+        w2_round(1, 1, AT_LAST_W2_ROUNDED, nc.scalar.copy)
+        w2_quantise(1, 0)
         for t in range(PACK):
-            z_row(0, t, 0, M, on_vector=(t == last))
-
-        w3_rounded = sbuf("w3_rounded", [P, 2, N, PACK], BF16)
-        nc.scalar.copy(
+            product(0, t, 0, M)
+        w2_quantise(1, 1)
+        for t in range(2):
+            z_row(0, t, 0, M)
+        for t in range(PACK):
+            b_tile(1, t, 0, M)
+        for t in range(2, PACK):
+            z_row(0, t, 0, M)
+        w3_rounded = sbuf("w3_rounded", [P, 2, N, PACK], BF16, AT_LAST_W2_ROUNDED)
+        nc.vector.tensor_copy(
             w3_rounded[:].rearrange("p c (f i) t -> p c f t i", i=4),
             w3_raw[:].rearrange("p c t (f i) -> p c f t i", i=4),
         )
         nc.vector.quantize_mx(
             out=w3_c[:].bitcast(FP8X4), scales=w3_s[:], in_=w3_rounded[:].rearrange("p c n t -> p (c n t)")
         )
-        z_quantise(0, 0, M, nc.scalar.copy, AT_LAST_W2_CODES)
-
-        def z_half(m0, m1):
-            for t in range(PACK):
-                product(1, t, m0, m1)
-                z_row(1, t, m0, m1)
-            z_quantise(1, m0, m1, nc.vector.tensor_copy)
-
-        m0, m1 = HALVES[0]
-        z_half(m0, m1)
-        acc = psum.tile([P, BANK], F32, name="acc", bufs=ACC_BANKS)
-        for n in range(2):
-            scores(acc[:, (m1 - m0) * n : (m1 - m0) * (n + 1)], n, m0, m1)
-        first = sbuf("first", [P, 2, m1 - m0], F32)
-        nc.scalar.copy(first[:].rearrange("p n m -> p (n m)"), acc[:])
-        nc.sync.dma_start(out[:, m0:m1].rearrange("(n p) m -> p n m", p=P), first[:])
-
-        m0, m1 = HALVES[1]
-        z_half(m0, m1)
-        for n, copy in enumerate((nc.scalar.copy, nc.vector.tensor_copy)):
-            acc = psum.tile([P, BANK], F32, name="acc", bufs=ACC_BANKS)
-            scores(acc[:, : m1 - m0], n, m0, m1)
-            second = sbuf("second%d" % n, [P, m1 - m0], F32)
-            copy(second[:], acc[:, : m1 - m0])
-            nc.sync.dma_start(out[P * n : P * (n + 1), m0:m1], second[:])
+        z_weave(0, 0, M, nc.scalar.copy)
+        z_quantise(0, 0, M)
+        for t in range(last):
+            product(1, t, 0, M)
+            z_row(1, t, 0, M)
+        banks = {}
+        for m0, m1 in HALVES:
+            for n in range(2):
+                banks[m0, n] = psum.tile([P, BANK], F32, name="acc", bufs=ACC_BANKS)
+                scores(banks[m0, n][:, : m1 - m0], n, m0, m1, (0,))
+        (a0, a1), (b0, b1) = HALVES
+        product(1, last, a0, a1)
+        z_row(1, last, a0, a1, on_vector=True)
+        z_weave(1, a0, a1, nc.scalar.copy)
+        product(1, last, b0, b1)
+        z_row(1, last, b0, b1, on_vector=True)
+        z_weave(1, b0, b1, nc.vector.tensor_copy)
+        for m0, m1 in reversed(HALVES):
+            z_quantise(1, m0, m1)
+            for n, copy in enumerate((nc.scalar.copy, nc.vector.tensor_copy)):
+                scores(banks[m0, n][:, : m1 - m0], n, m0, m1, (1,))
+        for m0, m1 in reversed(HALVES):
+            done = sbuf("done%d" % m0, [P, 2, m1 - m0], F32)
+            for n, copy in enumerate((nc.scalar.copy, nc.vector.tensor_copy)):
+                copy(done[:, n, :], banks[m0, n][:, : m1 - m0])
+            nc.sync.dma_start(out[:, m0:m1].rearrange("(n p) m -> p n m", p=P), done[:])

@@ -31,16 +31,16 @@ V_AT, W1_AT, V2_AT = 0, S, S + H
 HALVES = [(0, M // 2), (M // 2, M)]
 
 KIB = 1024
-AT_TAB = (4 * KIB, 25 * KIB)
-AT_W2 = {(0, 0): 0, (0, 1): 9 * KIB, (1, 0): 33 * KIB, (1, 1): 0 * KIB}
+AT_TAB = (4 * KIB, 27 * KIB)
+AT_W2 = {(0, 0): 0, (0, 1): 11 * KIB, (1, 0): 19 * KIB, (1, 1): 0 * KIB}
 AT_GAIN = 8 * KIB
-AT_TAB2 = (17 * KIB, 25 * KIB)
-AT_W3 = 9 * KIB
-AT_W1_CODES = 41 * KIB
-AT_V_CODES = 45 * KIB
+AT_TAB2 = (27 * KIB, 35 * KIB)
+AT_W3 = 11 * KIB
+AT_W1_CODES = 43 * KIB
+AT_V_CODES = 47 * KIB
 AT_V2_SCALES = AT_V_CODES - M // 2
-AT_LAST_W2_CODES = 49 * KIB
-AT_LAST_W2_ROUNDED = 53 * KIB
+AT_LAST_W2_CODES = 51 * KIB
+AT_LAST_W2_ROUNDED = 55 * KIB
 
 
 def tile_list_stemma_innovation_scores_kernel(
@@ -78,11 +78,16 @@ def tile_list_stemma_innovation_scores_kernel(
         nc.sync.dma_start(w1_s_raw[:].bitcast(I32), w1_scales.rearrange("a q c -> (a q) c").bitcast(I32))
         p1 = lists.tile([P, M // LIST_ROWS], U16, name="p1")
         nc.sync.dma_start(p1[:], pos1)
-        w1_raw = sbuf("w1_raw", [P, 4 * H], U8)
-        nc.sync.dma_start(
-            w1_raw[:].bitcast(I32).rearrange("p (a c) -> p a c", a=2),
-            w1_words.bitcast(I32).rearrange("a p c -> p a c"),
-        )
+        w1_raw = {}
+
+        def w1_load(c, at=None):
+            w1_raw[c] = sbuf("w1_raw%d" % c, [P, 2 * H], U8, at)
+            nc.sync.dma_start(
+                w1_raw[c][:].bitcast(I32).rearrange("p (a c) -> p a c", a=2),
+                w1_words.bitcast(I32).rearrange("a p c -> p a c")[:, :, H // 4 * c : H // 4 * (c + 1)],
+            )
+
+        w1_load(0)
         tab_w = []
         for a in range(2):
             tab_w.append(sbuf("tab_w%d" % a, [P, T], I32, AT_TAB[a]))
@@ -105,11 +110,16 @@ def tile_list_stemma_innovation_scores_kernel(
                 row = 16 * a + 4 * u
                 queue.dma_start(planes[a][32 * u : 32 * u + 4, :].bitcast(I32), staged[row : row + 4, :].bitcast(I32))
 
-        w1_c = sbuf("w1_c", [P, 4 * H], U8, AT_W1_CODES)
-        nc.vector.tensor_copy(
-            w1_c[:].bitcast(I32).rearrange("p (c t g e) -> p c t g e", t=PACK, g=16, e=4),
-            w1_raw[:].bitcast(I32).rearrange("p (c g t e) -> p c t g e", t=PACK, g=16, e=4),
-        )
+        w1_c = {}
+
+        def w1_order(c, at=None):
+            w1_c[c] = sbuf("w1_c%d" % c, [P, 2 * H], U8, at)
+            nc.vector.tensor_copy(
+                w1_c[c][:].bitcast(I32).rearrange("p (a t g e) -> p a t g e", t=PACK, g=16, e=4),
+                w1_raw[c][:].bitcast(I32).rearrange("p (a g t e) -> p a t g e", t=PACK, g=16, e=4),
+            )
+
+        w1_order(0, AT_W1_CODES + 2 * KIB)
 
         v_c0 = sbuf("v_c0", [P, S], U32, AT_V_CODES)
         nc.vector.tensor_copy(v_c0[:], tab_w[0][:].bitcast(U32).indirect(idx[:]))
@@ -132,6 +142,7 @@ def tile_list_stemma_innovation_scores_kernel(
             )
 
         w2_load(0, 0)
+        w1_load(1, 8 * KIB + 512)
         w2_load(0, 1)
         tab2_w = {}
 
@@ -147,6 +158,7 @@ def tile_list_stemma_innovation_scores_kernel(
                     nc.sync.dma_start(raw[:, c, t, :], w3_rows[c, t])
             return raw
 
+        w2_load(1, 0)
         tab2_load(0)
         tab2_load(1)
         gain_rows = sbuf("gain_rows", [P, P], F32, AT_GAIN)
@@ -158,7 +170,7 @@ def tile_list_stemma_innovation_scores_kernel(
             )
         ident = sbuf("ident", [P, P], F32)
         make_identity(nc, ident[:])
-        w2_load(1, 0)
+
 
         tanh_x1 = {}
 
@@ -168,14 +180,15 @@ def tile_list_stemma_innovation_scores_kernel(
             col = PASS * c + P * t
             if True:
                 acc = psum.tile([P, BANK], F32, name="acc", bufs=ACC_BANKS)
-                for a in range(2):
+                passes = (0, 1) if (c, h) == (0, 0) and t < 2 else (1, 0)
+                for a in passes:
                     nc.tensor.matmul_mx(
                         out=acc[:],
-                        lhsT=w1_c[:, 2 * (H * a + col) : 2 * (H * a + col + P)].bitcast(FP4X4),
+                        lhsT=w1_c[c][:, 2 * (PASS * a + P * t) : 2 * (PASS * a + P * (t + 1))].bitcast(FP4X4),
                         lhsT_scale=planes[a][:, W1_AT + col : W1_AT + col + P],
                         rhs=v_c[a, h].bitcast(FP8X4),
                         rhs_scale=planes[a][:, V_AT + BANK * h : V_AT + BANK * (h + 1)],
-                        start=(a == 0), stop=(a == 1),
+                        start=(a == passes[0]), stop=(a == passes[1]),
                     )
                 nc.scalar.activation(tanh_x1[c, t][:, BANK * h : BANK * (h + 1)], acc[:], ACT.Tanh, scale=0.5)
 
@@ -238,7 +251,7 @@ def tile_list_stemma_innovation_scores_kernel(
 
         def z_row(c, t, m0, m1, on_vector=False):
             if c not in z_rows:
-                z_rows[c] = sbuf("z_rows%d" % c, [P, PACK, M], BF16)
+                z_rows[c] = sbuf("z_rows%d" % c, [P, PACK, M], BF16, AT_TAB2[0] if c == 0 else None)
             level = half_gain[:, PACK * c + t : PACK * c + t + 1]
             slope = level
             if on_vector:
@@ -289,15 +302,17 @@ def tile_list_stemma_innovation_scores_kernel(
                 for t in (t0, t0 + 1):
                     x1_bank(0, t, h)
         w2_round(0, 0)
+        w1_order(1)
         w2_load(1, 1)
         w2_round(0, 1)
         w3_raw = w3_load()
         w2_quantise(0, 0)
         w2_quantise(0, 1)
+        w2_round(1, 0)
         v2_gather(0)
+        w2_quantise(1, 0)
         v2_gather(1)
-        pick(0)
-        pick(1)
+        pick(0, AT_TAB2[1])
         for t in range(PACK):
             for h in range(2):
                 x1_bank(1, t, h)
@@ -307,31 +322,29 @@ def tile_list_stemma_innovation_scores_kernel(
         nc.tensor.transpose(turned[:, :P], gain_rows[:], ident[:])
         half_gain = sbuf("half_gain", [P, 2 * PACK], F32)
         nc.vector.tensor_scalar(half_gain[:], turned[:, : 2 * PACK], 0.5, None, ALU.mult)
-        w2_round(1, 0)
-        w2_round(1, 1, AT_LAST_W2_ROUNDED, nc.scalar.copy)
-        w2_quantise(1, 0)
-        for t in range(PACK):
-            product(0, t, 0, M)
+        w2_round(1, 1, AT_LAST_W2_ROUNDED)
         w2_quantise(1, 1)
-        for t in range(2):
-            z_row(0, t, 0, M)
         for t in range(PACK):
             b_tile(1, t, 0, M)
-        for t in range(2, PACK):
+        product(0, 0, 0, M, AT_W2[1, 1])
+        product(0, 1, 0, M, AT_LAST_W2_ROUNDED)
+        product(0, 2, 0, M, AT_LAST_W2_ROUNDED + 2 * KIB)
+        product(0, 3, 0, M, AT_W2[1, 1] + 2 * KIB)
+        for t in range(PACK):
             z_row(0, t, 0, M)
-        w3_rounded = sbuf("w3_rounded", [P, 2, N, PACK], BF16, AT_LAST_W2_ROUNDED)
-        nc.vector.tensor_copy(
+        z_weave(0, 0, M, nc.scalar.copy)
+        w3_rounded = sbuf("w3_rounded", [P, 2, N, PACK], BF16)
+        nc.scalar.copy(
             w3_rounded[:].rearrange("p c (f i) t -> p c f t i", i=4),
             w3_raw[:].rearrange("p c t (f i) -> p c f t i", i=4),
         )
         nc.vector.quantize_mx(
             out=w3_c[:].bitcast(FP8X4), scales=w3_s[:], in_=w3_rounded[:].rearrange("p c n t -> p (c n t)")
         )
-        z_weave(0, 0, M, nc.scalar.copy)
         z_quantise(0, 0, M)
         for t in range(last):
             product(1, t, 0, M)
-            z_row(1, t, 0, M)
+            z_row(1, t, 0, M, on_vector=(t > 0))
         banks = {}
         for m0, m1 in HALVES:
             for n in range(2):
@@ -340,7 +353,7 @@ def tile_list_stemma_innovation_scores_kernel(
         (a0, a1), (b0, b1) = HALVES
         product(1, last, a0, a1)
         z_row(1, last, a0, a1, on_vector=True)
-        z_weave(1, a0, a1, nc.scalar.copy)
+        z_weave(1, a0, a1, nc.scalar.copy, AT_TAB2[0])
         product(1, last, b0, b1)
         z_row(1, last, b0, b1, on_vector=True)
         z_weave(1, b0, b1, nc.vector.tensor_copy)

@@ -24,7 +24,10 @@ RUN = 8
 BANK = 512
 LIST_ROWS = 16
 SCALE_ROWS = 32
+BLOCKS = 16
 ACC_BANKS = 6
+EARLY_BANKS = 2
+EARLY_PICKS = 2
 
 V_AT, W1_AT, V2_AT = 0, S, S + H
 
@@ -32,11 +35,11 @@ HALVES = [(0, M // 2), (M // 2, M)]
 
 KIB = 1024
 AT_TAB = (4 * KIB, 27 * KIB)
-AT_W2 = {(0, 0): 0, (0, 1): 11 * KIB, (1, 0): 19 * KIB, (1, 1): 0 * KIB}
-AT_GAIN = 8 * KIB
+AT_W2_BLOCK = 0
+AT_W1_SECOND = 8 * KIB + 512
+AT_W2_ROWS = 11 * KIB
 AT_TAB2 = (27 * KIB, 35 * KIB)
-AT_W3 = 11 * KIB
-AT_W1_CODES = 43 * KIB
+AT_W1_CODES = 45 * KIB
 AT_V_CODES = 47 * KIB
 AT_V2_SCALES = AT_V_CODES - M // 2
 AT_LAST_W2_CODES = 51 * KIB
@@ -62,9 +65,9 @@ def tile_list_stemma_innovation_scores_kernel(
         tab_s = sbuf("tab_s", [P, T], U8)
         tab2_s = sbuf("tab2_s", [P, T2], U8)
         w1_s_raw = sbuf("w1_s_raw", [SCALE_ROWS, H], U8)
-        for rows in (tab_s, tab2_s):
-            nc.vector.memset(rows[32:64, :].bitcast(I32), 0)
-            nc.vector.memset(rows[64:128, :].bitcast(I32), 0)
+        for rows, engine in ((tab_s, nc.vector), (tab2_s, nc.gpsimd)):
+            engine.memset(rows[32:64, :].bitcast(I32), 0)
+            engine.memset(rows[64:128, :].bitcast(I32), 0)
         planes = [sbuf("planes%d" % a, [P, S + H + M], U8) for a in range(2)]
         for a in range(2):
             nc.gpsimd.memset(planes[a][:].bitcast(I32), 0)
@@ -100,8 +103,8 @@ def tile_list_stemma_innovation_scores_kernel(
         staged = planes[0][:SCALE_ROWS, :]
         nc.vector.tensor_copy(staged[:, V_AT:W1_AT].bitcast(I32), v_s[:SCALE_ROWS, :].bitcast(I32))
         nc.vector.tensor_copy(
-            staged[:, W1_AT:V2_AT].bitcast(I32).rearrange("p (c t g e) -> p c t g e", t=PACK, g=16, e=2),
-            w1_s_raw[:].bitcast(I32).rearrange("p (c g t e) -> p c t g e", t=PACK, g=16, e=2),
+            staged[:, W1_AT:V2_AT].bitcast(I32).rearrange("p (c t g e) -> p c t g e", t=PACK, g=BLOCKS, e=2),
+            w1_s_raw[:].bitcast(I32).rearrange("p (c g t e) -> p c t g e", t=PACK, g=BLOCKS, e=2),
         )
         nc.vector.tensor_copy(staged[:, V2_AT:].bitcast(I32), v2_s[:SCALE_ROWS, :].bitcast(I32))
         for a in range(2):
@@ -115,11 +118,11 @@ def tile_list_stemma_innovation_scores_kernel(
         def w1_order(c, at=None):
             w1_c[c] = sbuf("w1_c%d" % c, [P, 2 * H], U8, at)
             nc.vector.tensor_copy(
-                w1_c[c][:].bitcast(I32).rearrange("p (a t g e) -> p a t g e", t=PACK, g=16, e=4),
-                w1_raw[c][:].bitcast(I32).rearrange("p (a g t e) -> p a t g e", t=PACK, g=16, e=4),
+                w1_c[c][:].bitcast(I32).rearrange("p (a t g e) -> p a t g e", t=PACK, g=BLOCKS, e=4),
+                w1_raw[c][:].bitcast(I32).rearrange("p (a g t e) -> p a t g e", t=PACK, g=BLOCKS, e=4),
             )
 
-        w1_order(0, AT_W1_CODES + 2 * KIB)
+        w1_order(0, AT_W1_CODES)
 
         v_c0 = sbuf("v_c0", [P, S], U32, AT_V_CODES)
         nc.vector.tensor_copy(v_c0[:], tab_w[0][:].bitcast(U32).indirect(idx[:]))
@@ -127,50 +130,31 @@ def tile_list_stemma_innovation_scores_kernel(
         for h in range(2):
             v_c[0, h] = v_c0[:, BANK * h : BANK * (h + 1)]
         for h in range(2):
-            half = sbuf("v_c1%d" % h, [P, BANK], U32)
+            gathered = sbuf("v_c1%d" % h, [P, BANK], U32)
             entries = idx[:, BANK * h // LIST_ROWS : BANK * (h + 1) // LIST_ROWS]
-            nc.vector.tensor_copy(half[:], tab_w[1][:].bitcast(U32).indirect(entries))
-            v_c[1, h] = half[:]
+            nc.vector.tensor_copy(gathered[:], tab_w[1][:].bitcast(U32).indirect(entries))
+            v_c[1, h] = gathered[:]
 
         w2_raw = {}
 
-        def w2_load(c, a):
-            w2_raw[c, a] = sbuf("w2_raw%d%d" % (c, a), [P, PACK, PASS], F32, AT_W2[c, a])
+        def w2_load_block(c):
+            w2_raw[c, 0] = sbuf("w2_raw%d0" % c, [P, PACK, PASS], F32, AT_W2_BLOCK)
             nc.sync.dma_start(
-                w2_raw[c, a][:],
-                w2[PASS * a : PASS * (a + 1), PASS * c : PASS * (c + 1)].rearrange("(p i) r -> p i r", i=PACK),
+                w2_raw[c, 0][:], w2[:PASS, PASS * c : PASS * (c + 1)].rearrange("(p i) r -> p i r", i=PACK)
             )
 
-        w2_load(0, 0)
-        w1_load(1, 8 * KIB + 512)
-        w2_load(0, 1)
-        tab2_w = {}
-
-        def tab2_load(a):
-            tab2_w[a] = sbuf("tab2_w%d" % a, [P, T2], I32, AT_TAB2[a])
-            nc.sync.dma_start(tab2_w[a][:], tab2_words[a].rearrange("p t i -> p (t i)").bitcast(I32))
-
-        def w3_load():
-            raw = sbuf("w3_raw", [P, 2, PACK, N], F32, AT_W3)
-            w3_rows = w3.rearrange("(c g t e) n -> c t g e n", c=2, t=PACK, e=RUN)
-            for c in range(2):
-                for t in range(PACK):
-                    nc.sync.dma_start(raw[:, c, t, :], w3_rows[c, t])
-            return raw
-
-        w2_load(1, 0)
-        tab2_load(0)
-        tab2_load(1)
-        gain_rows = sbuf("gain_rows", [P, P], F32, AT_GAIN)
-        nc.gpsimd.memset(gain_rows[:], 0.0)
+        w2_load_block(0)
+        w1_load(1, AT_W1_SECOND)
+        w2_rows = sbuf("w2_rows", [P, PACK, H], F32, AT_W2_ROWS)
+        nc.sync.dma_start(w2_rows[:], w2[PASS:, :].rearrange("(p i) r -> p i r", i=PACK))
         for c in range(2):
-            nc.sync.dma_start(
-                gain_rows[PACK * c : PACK * (c + 1), :].rearrange("t (g e) -> t g e", e=RUN),
-                gain.rearrange("(c g t e) -> c t g e", c=2, t=PACK, e=RUN)[c],
-            )
+            w2_raw[c, 1] = w2_rows[:, :, PASS * c : PASS * (c + 1)]
+        tab2_w = []
+        for a in range(2):
+            tab2_w.append(sbuf("tab2_w%d" % a, [P, T2], I32, AT_TAB2[a]))
+            nc.sync.dma_start(tab2_w[a][:], tab2_words[a].rearrange("p t i -> p (t i)").bitcast(I32))
         ident = sbuf("ident", [P, P], F32)
         make_identity(nc, ident[:])
-
 
         tanh_x1 = {}
 
@@ -178,25 +162,24 @@ def tile_list_stemma_innovation_scores_kernel(
             if h == 0:
                 tanh_x1[c, t] = sbuf("tanh_x1_%d%d" % (c, t), [P, S], F32)
             col = PASS * c + P * t
-            if True:
-                acc = psum.tile([P, BANK], F32, name="acc", bufs=ACC_BANKS)
-                passes = (0, 1) if (c, h) == (0, 0) and t < 2 else (1, 0)
-                for a in passes:
-                    nc.tensor.matmul_mx(
-                        out=acc[:],
-                        lhsT=w1_c[c][:, 2 * (PASS * a + P * t) : 2 * (PASS * a + P * (t + 1))].bitcast(FP4X4),
-                        lhsT_scale=planes[a][:, W1_AT + col : W1_AT + col + P],
-                        rhs=v_c[a, h].bitcast(FP8X4),
-                        rhs_scale=planes[a][:, V_AT + BANK * h : V_AT + BANK * (h + 1)],
-                        start=(a == passes[0]), stop=(a == passes[1]),
-                    )
-                nc.scalar.activation(tanh_x1[c, t][:, BANK * h : BANK * (h + 1)], acc[:], ACT.Tanh, scale=0.5)
+            acc = psum.tile([P, BANK], F32, name="acc", bufs=ACC_BANKS)
+            k_passes = (0, 1) if (c, h) == (0, 0) and t < EARLY_BANKS else (1, 0)
+            for a in k_passes:
+                nc.tensor.matmul_mx(
+                    out=acc[:],
+                    lhsT=w1_c[c][:, 2 * (PASS * a + P * t) : 2 * (PASS * a + P * (t + 1))].bitcast(FP4X4),
+                    lhsT_scale=planes[a][:, W1_AT + col : W1_AT + col + P],
+                    rhs=v_c[a, h].bitcast(FP8X4),
+                    rhs_scale=planes[a][:, V_AT + BANK * h : V_AT + BANK * (h + 1)],
+                    start=(a == k_passes[0]), stop=(a == k_passes[1]),
+                )
+            nc.scalar.activation(tanh_x1[c, t][:, BANK * h : BANK * (h + 1)], acc[:], ACT.Tanh, scale=0.5)
 
         w2_rounded, w2_c, w2_s = {}, {}, {}
 
-        def w2_round(c, a, at=None, copy=nc.vector.tensor_copy):
+        def w2_round(c, a, at=None):
             w2_rounded[c, a] = sbuf("w2_rounded%d%d" % (c, a), [P, PACK, P, PACK], BF16, at)
-            copy(
+            nc.vector.tensor_copy(
                 w2_rounded[c, a][:].rearrange("p t (g e) i -> p t g e i", e=RUN),
                 w2_raw[c, a][:].rearrange("p i (g t e) -> p t g e i", t=PACK, e=RUN),
             )
@@ -217,123 +200,132 @@ def tile_list_stemma_innovation_scores_kernel(
 
         tanh_b = {}
 
-        def b_tile(c, t, m0, m1):
+        def b_tile(c, t):
             acc = psum.tile([P, BANK], F32, name="acc", bufs=ACC_BANKS)
             for a in range(2):
                 nc.tensor.matmul_mx(
-                    out=acc[:, : m1 - m0],
+                    out=acc[:],
                     lhsT=w2_c[c, a][:, P * t : P * (t + 1)].bitcast(FP8X4),
                     lhsT_scale=w2_s[c, a][:, P * t : P * (t + 1)],
-                    rhs=v2_c[a][:, m0:m1].bitcast(FP8X4),
-                    rhs_scale=planes[a][:, V2_AT + m0 : V2_AT + m1],
+                    rhs=v2_c[a][:].bitcast(FP8X4),
+                    rhs_scale=planes[a][:, V2_AT : V2_AT + M],
                     start=(a == 0), stop=(a == 1),
                 )
-            tanh_b[c, t, m0] = sbuf("tanh_b%d%d_%d" % (c, t, m0), [P, m1 - m0], F32)
-            nc.scalar.activation(tanh_b[c, t, m0][:], acc[:, : m1 - m0], ACT.Tanh, scale=-0.5)
+            tanh_b[c, t] = sbuf("tanh_b%d%d" % (c, t), [P, M], F32)
+            nc.scalar.activation(tanh_b[c, t][:], acc[:], ACT.Tanh, scale=-0.5)
 
         picked = {}
 
-        def pick(t, at=None):
-            picked[t] = sbuf("picked%d" % t, [P, M], F32, at)
-            nc.vector.tensor_copy(picked[t][:], tanh_x1[0, t][:].indirect(p1[:]))
+        def pick(c, t):
+            picked[c, t] = sbuf("picked%d%d" % (c, t), [P, M], F32)
+            nc.vector.tensor_copy(picked[c, t][:], tanh_x1[c, t][:].indirect(p1[:]))
 
         products = {}
 
         def product(c, t, m0, m1, at=None):
             products[c, t, m0] = sbuf("product%d%d_%d" % (c, t, m0), [P, m1 - m0], F32, at)
-            if c == 0 and t in picked:
-                exemplar = picked[t][:, m0:m1]
+            if (c, t) in picked:
+                exemplar = picked[c, t][:, m0:m1]
             else:
                 exemplar = tanh_x1[c, t][:].indirect(p1[:, m0 // LIST_ROWS : m1 // LIST_ROWS])
-            nc.vector.tensor_tensor(products[c, t, m0][:], exemplar, tanh_b[c, t, 0][:, m0:m1], ALU.mult)
+            nc.vector.tensor_tensor(products[c, t, m0][:], exemplar, tanh_b[c, t][:, m0:m1], ALU.mult)
 
         z_rows = {}
 
         def z_row(c, t, m0, m1, on_vector=False):
             if c not in z_rows:
                 z_rows[c] = sbuf("z_rows%d" % c, [P, PACK, M], BF16, AT_TAB2[0] if c == 0 else None)
-            level = half_gain[:, PACK * c + t : PACK * c + t + 1]
-            slope = level
+            factor = half_gain[:, PACK * c + t : PACK * c + t + 1]
             if on_vector:
-                nc.vector.tensor_scalar(z_rows[c][:, t, m0:m1], products[c, t, m0][:], slope, level, ALU.mult, ALU.add)
+                nc.vector.tensor_scalar(z_rows[c][:, t, m0:m1], products[c, t, m0][:], factor, factor, ALU.mult, ALU.add)
             else:
                 nc.scalar.activation(
-                    z_rows[c][:, t, m0:m1], products[c, t, m0][:], ACT.Identity, scale=slope, bias=level
+                    z_rows[c][:, t, m0:m1], products[c, t, m0][:], ACT.Identity, scale=factor, bias=factor
                 )
 
         z_c = [sbuf("z_c%d" % c, [P, M], U32) for c in range(2)]
         z_s = [sbuf("z_s%d" % c, [P, M], U8) for c in range(2)]
 
-        woven_of = {}
+        z_woven = {}
 
         def z_weave(c, m0, m1, copy, at=None):
-            woven = sbuf("z_woven%d_%d" % (c, m0), [P, m1 - m0, PACK], BF16, at)
+            z_woven[c, m0] = sbuf("z_woven%d_%d" % (c, m0), [P, m1 - m0, PACK], BF16, at)
             copy(
-                woven[:].rearrange("p (f i) t -> p f t i", i=4),
+                z_woven[c, m0][:].rearrange("p (f i) t -> p f t i", i=4),
                 z_rows[c][:, :, m0:m1].rearrange("p t (f i) -> p f t i", i=4),
             )
-            woven_of[c, m0] = woven
 
         def z_quantise(c, m0, m1):
-            woven = woven_of[c, m0]
             nc.vector.quantize_mx(
                 out=z_c[c][:, m0:m1].bitcast(FP8X4), scales=z_s[c][:, m0:m1],
-                in_=woven[:].rearrange("p m t -> p (m t)"),
+                in_=z_woven[c, m0][:].rearrange("p m t -> p (m t)"),
             )
 
         w3_c = sbuf("w3_c", [P, 2 * N], U32)
         w3_s = sbuf("w3_s", [P, 2 * N], U8)
 
-        def scores(acc, n, m0, m1, passes=(0, 1)):
-            for c in passes:
-                cols = slice(N * c + P * n, N * c + P * (n + 1))
-                nc.tensor.matmul_mx(
-                    out=acc,
-                    lhsT=w3_c[:, cols].bitcast(FP8X4),
-                    lhsT_scale=w3_s[:, cols],
-                    rhs=z_c[c][:, m0:m1].bitcast(FP8X4),
-                    rhs_scale=z_s[c][:, m0:m1],
-                    start=(c == 0), stop=(c == 1),
-                )
+        def scores(acc, c, n, m0, m1):
+            cols = slice(N * c + P * n, N * c + P * (n + 1))
+            nc.tensor.matmul_mx(
+                out=acc,
+                lhsT=w3_c[:, cols].bitcast(FP8X4),
+                lhsT_scale=w3_s[:, cols],
+                rhs=z_c[c][:, m0:m1].bitcast(FP8X4),
+                rhs_scale=z_s[c][:, m0:m1],
+                start=(c == 0), stop=(c == 1),
+            )
 
-        last = PACK - 1
-        for t0 in (0, 2):
+        for t0 in range(0, PACK, 2):
             for h in range(2):
                 for t in (t0, t0 + 1):
                     x1_bank(0, t, h)
+
         w2_round(0, 0)
         w1_order(1)
-        w2_load(1, 1)
-        w2_round(0, 1)
-        w3_raw = w3_load()
+        w2_load_block(1)
+        gain_rows = sbuf("gain_rows", [P, P], F32, AT_W1_SECOND)
+        nc.gpsimd.memset(gain_rows[:], 0.0)
+        for c in range(2):
+            nc.sync.dma_start(
+                gain_rows[PACK * c : PACK * (c + 1), :].rearrange("t (g e) -> t g e", e=RUN),
+                gain.rearrange("(c g t e) -> c t g e", c=2, t=PACK, e=RUN)[c],
+            )
         w2_quantise(0, 0)
-        w2_quantise(0, 1)
-        w2_round(1, 0)
-        v2_gather(0)
-        w2_quantise(1, 0)
-        v2_gather(1)
-        pick(0, AT_TAB2[1])
+        for t in range(EARLY_PICKS):
+            pick(0, t)
+        for c in range(2):
+            w2_round(c, 1)
+        w3_raw = sbuf("w3_raw", [P, 2, PACK, N], F32, AT_W2_ROWS)
+        w3_rows = w3.rearrange("(c g t e) n -> c t g e n", c=2, t=PACK, e=RUN)
+        for c in range(2):
+            for t in range(PACK):
+                nc.sync.dma_start(w3_raw[:, c, t, :], w3_rows[c, t])
+        for c in range(2):
+            w2_quantise(c, 1)
+        for a in range(2):
+            v2_gather(a)
+
         for t in range(PACK):
             for h in range(2):
                 x1_bank(1, t, h)
         for t in range(PACK):
-            b_tile(0, t, 0, M)
-        turned = psum.tile([P, BANK], F32, name="late", bufs=2)
+            b_tile(0, t)
+        turned = psum.tile([P, BANK], F32, name="turned")
         nc.tensor.transpose(turned[:, :P], gain_rows[:], ident[:])
         half_gain = sbuf("half_gain", [P, 2 * PACK], F32)
         nc.vector.tensor_scalar(half_gain[:], turned[:, : 2 * PACK], 0.5, None, ALU.mult)
-        w2_round(1, 1, AT_LAST_W2_ROUNDED)
-        w2_quantise(1, 1)
+        w2_round(1, 0, AT_LAST_W2_ROUNDED)
+        w2_quantise(1, 0, AT_LAST_W2_CODES)
         for t in range(PACK):
-            b_tile(1, t, 0, M)
-        product(0, 0, 0, M, AT_W2[1, 1])
-        product(0, 1, 0, M, AT_LAST_W2_ROUNDED)
-        product(0, 2, 0, M, AT_LAST_W2_ROUNDED + 2 * KIB)
-        product(0, 3, 0, M, AT_W2[1, 1] + 2 * KIB)
+            b_tile(1, t)
+
+        at_product = (AT_W2_BLOCK, AT_LAST_W2_ROUNDED, AT_LAST_W2_ROUNDED + 2 * KIB, AT_W2_BLOCK + 2 * KIB)
+        for t in range(PACK):
+            product(0, t, 0, M, at_product[t])
         for t in range(PACK):
             z_row(0, t, 0, M)
         z_weave(0, 0, M, nc.scalar.copy)
-        w3_rounded = sbuf("w3_rounded", [P, 2, N, PACK], BF16)
+        w3_rounded = sbuf("w3_rounded", [P, 2, N, PACK], BF16, AT_LAST_W2_CODES)
         nc.scalar.copy(
             w3_rounded[:].rearrange("p c (f i) t -> p c f t i", i=4),
             w3_raw[:].rearrange("p c t (f i) -> p c f t i", i=4),
@@ -342,6 +334,8 @@ def tile_list_stemma_innovation_scores_kernel(
             out=w3_c[:].bitcast(FP8X4), scales=w3_s[:], in_=w3_rounded[:].rearrange("p c n t -> p (c n t)")
         )
         z_quantise(0, 0, M)
+
+        last = PACK - 1
         for t in range(last):
             product(1, t, 0, M)
             z_row(1, t, 0, M, on_vector=(t > 0))
@@ -349,20 +343,18 @@ def tile_list_stemma_innovation_scores_kernel(
         for m0, m1 in HALVES:
             for n in range(2):
                 banks[m0, n] = psum.tile([P, BANK], F32, name="acc", bufs=ACC_BANKS)
-                scores(banks[m0, n][:, : m1 - m0], n, m0, m1, (0,))
-        (a0, a1), (b0, b1) = HALVES
-        product(1, last, a0, a1)
-        z_row(1, last, a0, a1, on_vector=True)
-        z_weave(1, a0, a1, nc.scalar.copy, AT_TAB2[0])
-        product(1, last, b0, b1)
-        z_row(1, last, b0, b1, on_vector=True)
-        z_weave(1, b0, b1, nc.vector.tensor_copy)
+                scores(banks[m0, n][:, : m1 - m0], 0, n, m0, m1)
+        for (m0, m1), copy, at in zip(HALVES, (nc.scalar.copy, nc.vector.tensor_copy), (AT_TAB2[0], None)):
+            product(1, last, m0, m1)
+            z_row(1, last, m0, m1, on_vector=True)
+            z_weave(1, m0, m1, copy, at)
+
         for m0, m1 in reversed(HALVES):
             z_quantise(1, m0, m1)
-            for n, copy in enumerate((nc.scalar.copy, nc.vector.tensor_copy)):
-                scores(banks[m0, n][:, : m1 - m0], n, m0, m1, (1,))
+            for n in range(2):
+                scores(banks[m0, n][:, : m1 - m0], 1, n, m0, m1)
         for m0, m1 in reversed(HALVES):
-            done = sbuf("done%d" % m0, [P, 2, m1 - m0], F32)
             for n, copy in enumerate((nc.scalar.copy, nc.vector.tensor_copy)):
-                copy(done[:, n, :], banks[m0, n][:, : m1 - m0])
-            nc.sync.dma_start(out[:, m0:m1].rearrange("(n p) m -> p n m", p=P), done[:])
+                done = sbuf("done%d_%d" % (m0, n), [P, m1 - m0], F32)
+                copy(done[:], banks[m0, n][:, : m1 - m0])
+                nc.sync.dma_start(out[P * n : P * (n + 1), m0:m1], done[:])

@@ -27,7 +27,7 @@ SCALE_ROWS = 32
 BLOCKS = 16
 ACC_BANKS = 6
 EARLY_BANKS = 2
-EARLY_PICKS = 2
+EARLY_PICKS = 3
 
 V_AT, W1_AT, V2_AT = 0, S, S + H
 
@@ -184,6 +184,15 @@ def tile_list_stemma_innovation_scores_kernel(
                 w2_raw[c, a][:].rearrange("p i (g t e) -> p t g e i", t=PACK, e=RUN),
             )
 
+        def w2_round_on_gpsimd(c, a):
+            w2_rounded[c, a] = sbuf("w2_rounded%d%d" % (c, a), [P, PACK, P, PACK], BF16)
+            for t in range(PACK):
+                nc.gpsimd.tensor_scalar(
+                    w2_rounded[c, a][:, t].rearrange("p (g e) i -> p g e i", e=RUN),
+                    w2_raw[c, a][:].rearrange("p i (g t e) -> p t g e i", t=PACK, e=RUN)[:, t],
+                    1.0, 0.0, ALU.mult, ALU.add,
+                )
+
         def w2_quantise(c, a, at=None):
             w2_c[c, a] = sbuf("w2_c%d%d" % (c, a), [P, PASS], U32, at)
             w2_s[c, a] = sbuf("w2_s%d%d" % (c, a), [P, PASS], U8)
@@ -293,17 +302,17 @@ def tile_list_stemma_innovation_scores_kernel(
         w2_quantise(0, 0)
         for t in range(EARLY_PICKS):
             pick(0, t)
-        for c in range(2):
-            w2_round(c, 1)
+        w2_round(0, 1)
+        w2_round_on_gpsimd(1, 1)
         w3_raw = sbuf("w3_raw", [P, 2, PACK, N], F32, AT_W2_ROWS)
         w3_rows = w3.rearrange("(c g t e) n -> c t g e n", c=2, t=PACK, e=RUN)
         for c in range(2):
             for t in range(PACK):
                 nc.sync.dma_start(w3_raw[:, c, t, :], w3_rows[c, t])
-        for c in range(2):
-            w2_quantise(c, 1)
+        w2_quantise(0, 1)
         for a in range(2):
             v2_gather(a)
+        w2_quantise(1, 1, AT_TAB2[1])
 
         for t in range(PACK):
             for h in range(2):

@@ -25,9 +25,9 @@ BANK = 512
 LIST_ROWS = 16
 SCALE_ROWS = 32
 BLOCKS = 16
-ACC_BANKS = 6
+ACC_BANKS = 7
 EARLY_BANKS = 2
-EARLY_PICKS = 3
+EARLY_PICKS = 4
 
 V_AT, W1_AT, V2_AT = 0, S, S + H
 
@@ -36,13 +36,16 @@ HALVES = [(0, M // 2), (M // 2, M)]
 KIB = 1024
 AT_TAB = (4 * KIB, 27 * KIB)
 AT_W2_BLOCK = 0
+AT_LAST_W2_RAW = AT_W2_BLOCK + 512
 AT_W1_SECOND = 8 * KIB + 512
 AT_W2_ROWS = 11 * KIB
 AT_TAB2 = (27 * KIB, 35 * KIB)
 AT_W1_CODES = 45 * KIB
 AT_V_CODES = 47 * KIB
 AT_V2_SCALES = AT_V_CODES - M // 2
-AT_LAST_W2_CODES = 51 * KIB
+AT_LAST_W2_CODES = 65 * KIB
+AT_Z_WOVEN = 61 * KIB
+AT_W3_ROUNDED = 68 * KIB
 AT_LAST_W2_ROUNDED = 55 * KIB
 
 
@@ -158,9 +161,9 @@ def tile_list_stemma_innovation_scores_kernel(
 
         tanh_x1 = {}
 
-        def x1_bank(c, t, h):
+        def x1_bank(c, t, h, at=None):
             if h == 0:
-                tanh_x1[c, t] = sbuf("tanh_x1_%d%d" % (c, t), [P, S], F32)
+                tanh_x1[c, t] = sbuf("tanh_x1_%d%d" % (c, t), [P, S], F32, at)
             col = PASS * c + P * t
             acc = psum.tile([P, BANK], F32, name="acc", bufs=ACC_BANKS)
             k_passes = (0, 1) if (c, h) == (0, 0) and t < EARLY_BANKS else (1, 0)
@@ -193,6 +196,14 @@ def tile_list_stemma_innovation_scores_kernel(
                     1.0, 0.0, ALU.mult, ALU.add,
                 )
 
+        def w2_round_on_scalar(c, a):
+            w2_rounded[c, a] = sbuf("w2_rounded%d%d" % (c, a), [P, PACK, P, PACK], BF16)
+            for t in range(PACK):
+                nc.scalar.copy(
+                    w2_rounded[c, a][:, t].rearrange("p (g u e) i -> p g u i e", u=2, e=4),
+                    w2_raw[c, a][:].rearrange("p i (g t u e) -> p t g u i e", t=PACK, u=2, e=4)[:, t],
+                )
+
         def w2_quantise(c, a, at=None):
             w2_c[c, a] = sbuf("w2_c%d%d" % (c, a), [P, PASS], U32, at)
             w2_s[c, a] = sbuf("w2_s%d%d" % (c, a), [P, PASS], U8)
@@ -209,19 +220,24 @@ def tile_list_stemma_innovation_scores_kernel(
 
         tanh_b = {}
 
-        def b_tile(c, t):
-            acc = psum.tile([P, BANK], F32, name="acc", bufs=ACC_BANKS)
-            for a in range(2):
-                nc.tensor.matmul_mx(
-                    out=acc[:],
-                    lhsT=w2_c[c, a][:, P * t : P * (t + 1)].bitcast(FP8X4),
-                    lhsT_scale=w2_s[c, a][:, P * t : P * (t + 1)],
-                    rhs=v2_c[a][:].bitcast(FP8X4),
-                    rhs_scale=planes[a][:, V2_AT : V2_AT + M],
-                    start=(a == 0), stop=(a == 1),
-                )
+        b_acc = {}
+
+        def b_pass(c, t, a):
+            first = (c, t) not in b_acc
+            if first:
+                b_acc[c, t] = psum.tile([P, BANK], F32, name="acc", bufs=ACC_BANKS)
+            nc.tensor.matmul_mx(
+                out=b_acc[c, t][:],
+                lhsT=w2_c[c, a][:, P * t : P * (t + 1)].bitcast(FP8X4),
+                lhsT_scale=w2_s[c, a][:, P * t : P * (t + 1)],
+                rhs=v2_c[a][:].bitcast(FP8X4),
+                rhs_scale=planes[a][:, V2_AT : V2_AT + M],
+                start=first, stop=not first,
+            )
+
+        def b_tanh(c, t):
             tanh_b[c, t] = sbuf("tanh_b%d%d" % (c, t), [P, M], F32)
-            nc.scalar.activation(tanh_b[c, t][:], acc[:], ACT.Tanh, scale=-0.5)
+            nc.scalar.activation(tanh_b[c, t][:], b_acc[c, t][:], ACT.Tanh, scale=-0.5)
 
         picked = {}
 
@@ -270,15 +286,28 @@ def tile_list_stemma_innovation_scores_kernel(
                 in_=z_woven[c, m0][:].rearrange("p m t -> p (m t)"),
             )
 
-        w3_c = sbuf("w3_c", [P, 2 * N], U32)
-        w3_s = sbuf("w3_s", [P, 2 * N], U8)
+        w3_rounded, w3_c, w3_s = {}, {}, {}
+
+        def w3_round(c, copy, at):
+            w3_rounded[c] = sbuf("w3_rounded%d" % c, [P, N, PACK], BF16, at)
+            copy(
+                w3_rounded[c][:].rearrange("p (f i) t -> p f t i", i=4),
+                w3_raw[c][:].rearrange("p t (f i) -> p f t i", i=4),
+            )
+
+        def w3_quantise(c):
+            w3_c[c] = sbuf("w3_c%d" % c, [P, N], U32)
+            w3_s[c] = sbuf("w3_s%d" % c, [P, N], U8)
+            nc.vector.quantize_mx(
+                out=w3_c[c][:].bitcast(FP8X4), scales=w3_s[c][:], in_=w3_rounded[c][:].rearrange("p n t -> p (n t)")
+            )
 
         def scores(acc, c, n, m0, m1):
-            cols = slice(N * c + P * n, N * c + P * (n + 1))
+            cols = slice(P * n, P * (n + 1))
             nc.tensor.matmul_mx(
                 out=acc,
-                lhsT=w3_c[:, cols].bitcast(FP8X4),
-                lhsT_scale=w3_s[:, cols],
+                lhsT=w3_c[c][:, cols].bitcast(FP8X4),
+                lhsT_scale=w3_s[c][:, cols],
                 rhs=z_c[c][:, m0:m1].bitcast(FP8X4),
                 rhs_scale=z_s[c][:, m0:m1],
                 start=(c == 0), stop=(c == 1),
@@ -291,8 +320,12 @@ def tile_list_stemma_innovation_scores_kernel(
 
         w2_round(0, 0)
         w1_order(1)
-        w2_load_block(1)
-        gain_rows = sbuf("gain_rows", [P, P], F32, AT_W1_SECOND)
+        last_raw = []
+        for u in range(2):
+            last_raw.append(sbuf("last_raw%d" % u, [P, PACK, PASS // 2], F32, AT_LAST_W2_RAW + 4 * KIB * u))
+            cols = slice(PASS + PASS // 2 * u, PASS + PASS // 2 * (u + 1))
+            nc.sync.dma_start(last_raw[u][:], w2[:PASS, cols].rearrange("(p i) r -> p i r", i=PACK))
+        gain_rows = sbuf("gain_rows", [P, P], F32, AT_W2_BLOCK)
         nc.gpsimd.memset(gain_rows[:], 0.0)
         for c in range(2):
             nc.sync.dma_start(
@@ -302,61 +335,76 @@ def tile_list_stemma_innovation_scores_kernel(
         w2_quantise(0, 0)
         for t in range(EARLY_PICKS):
             pick(0, t)
-        w2_round(0, 1)
-        w2_round_on_gpsimd(1, 1)
-        w3_raw = sbuf("w3_raw", [P, 2, PACK, N], F32, AT_W2_ROWS)
-        w3_rows = w3.rearrange("(c g t e) n -> c t g e n", c=2, t=PACK, e=RUN)
-        for c in range(2):
-            for t in range(PACK):
-                nc.sync.dma_start(w3_raw[:, c, t, :], w3_rows[c, t])
-        w2_quantise(0, 1)
-        for a in range(2):
-            v2_gather(a)
-        w2_quantise(1, 1, AT_TAB2[1])
-
-        for t in range(PACK):
+        for t in range(2):
             for h in range(2):
                 x1_bank(1, t, h)
+        w2_round_on_scalar(0, 1)
+        w2_round_on_gpsimd(1, 1)
+        w3_rows = w3.rearrange("(c g t e) n -> c t g e n", c=2, t=PACK, e=RUN)
+        w3_raw = []
+        for c in range(2):
+            w3_raw.append(sbuf("w3_raw%d" % c, [P, PACK, N], F32, AT_W2_ROWS + 4 * KIB * c))
+            for t in range(PACK):
+                nc.sync.dma_start(w3_raw[c][:, t, :], w3_rows[c, t])
+        v2_gather(0)
+        w2_quantise(0, 1, AT_TAB2[0] + 4 * KIB)
+        w2_quantise(1, 1, AT_TAB2[0] + 6 * KIB)
+        v2_gather(1)
+
+        for t in range(2, PACK):
+            for h in range(2):
+                x1_bank(1, t, h, AT_W2_ROWS + 4 * KIB * t)
         for t in range(PACK):
-            b_tile(0, t)
+            b_pass(0, t, 0)
+        for t in range(PACK):
+            b_pass(0, t, 1)
+            b_tanh(0, t)
         turned = psum.tile([P, BANK], F32, name="turned")
         nc.tensor.transpose(turned[:, :P], gain_rows[:], ident[:])
         half_gain = sbuf("half_gain", [P, 2 * PACK], F32)
         nc.vector.tensor_scalar(half_gain[:], turned[:, : 2 * PACK], 0.5, None, ALU.mult)
-        w2_round(1, 0, AT_LAST_W2_ROUNDED)
+        w2_rounded[1, 0] = sbuf("w2_rounded10", [P, PACK, P, PACK], BF16, AT_LAST_W2_ROUNDED)
+        for u in range(2):
+            nc.vector.tensor_copy(
+                w2_rounded[1, 0][:].rearrange("p t (u g e) i -> p u t g e i", u=2, e=RUN)[:, u],
+                last_raw[u][:].rearrange("p i (g t e) -> p t g e i", t=PACK, e=RUN),
+            )
         w2_quantise(1, 0, AT_LAST_W2_CODES)
         for t in range(PACK):
-            b_tile(1, t)
+            for a in (1, 0):
+                b_pass(1, t, a)
+            b_tanh(1, t)
 
-        at_product = (AT_W2_BLOCK, AT_LAST_W2_ROUNDED, AT_LAST_W2_ROUNDED + 2 * KIB, AT_W2_BLOCK + 2 * KIB)
+        at_product = (AT_LAST_W2_RAW + 4 * KIB, AT_LAST_W2_ROUNDED, AT_LAST_W2_ROUNDED + 2 * KIB, AT_LAST_W2_RAW + 6 * KIB)
         for t in range(PACK):
             product(0, t, 0, M, at_product[t])
         for t in range(PACK):
             z_row(0, t, 0, M)
-        z_weave(0, 0, M, nc.scalar.copy)
-        w3_rounded = sbuf("w3_rounded", [P, 2, N, PACK], BF16, AT_LAST_W2_CODES)
-        nc.scalar.copy(
-            w3_rounded[:].rearrange("p c (f i) t -> p c f t i", i=4),
-            w3_raw[:].rearrange("p c t (f i) -> p c f t i", i=4),
-        )
-        nc.vector.quantize_mx(
-            out=w3_c[:].bitcast(FP8X4), scales=w3_s[:], in_=w3_rounded[:].rearrange("p c n t -> p (c n t)")
-        )
-        z_quantise(0, 0, M)
+        z_weave(0, 0, M, nc.scalar.copy, AT_Z_WOVEN)
+        w3_round(1, nc.scalar.copy, AT_LAST_W2_CODES)
 
         last = PACK - 1
-        for t in range(last):
-            product(1, t, 0, M)
-            z_row(1, t, 0, M, on_vector=(t > 0))
+        product(1, 0, 0, M)
+        z_row(1, 0, 0, M)
+        w3_round(0, nc.vector.tensor_copy, AT_W3_ROUNDED)
+        product(1, 1, 0, M, AT_W2_ROWS)
+        w3_quantise(0)
+        product(1, 2, 0, M, AT_W2_ROWS + 2 * KIB)
+        z_row(1, 1, 0, M, on_vector=True)
+        product(1, last, *HALVES[0], AT_W3_ROUNDED)
+        z_row(1, 2, 0, M, on_vector=True)
+        product(1, last, *HALVES[1], AT_W3_ROUNDED + KIB)
+        z_row(1, last, *HALVES[0], on_vector=True)
+        z_quantise(0, 0, M)
+        z_row(1, last, *HALVES[1], on_vector=True)
         banks = {}
-        for m0, m1 in HALVES:
+        for m0, m1 in reversed(HALVES):
             for n in range(2):
                 banks[m0, n] = psum.tile([P, BANK], F32, name="acc", bufs=ACC_BANKS)
                 scores(banks[m0, n][:, : m1 - m0], 0, n, m0, m1)
-        for (m0, m1), copy, at in zip(HALVES, (nc.scalar.copy, nc.vector.tensor_copy), (AT_TAB2[0], None)):
-            product(1, last, m0, m1)
-            z_row(1, last, m0, m1, on_vector=True)
-            z_weave(1, m0, m1, copy, at)
+        z_weave(1, *HALVES[0], nc.scalar.copy, AT_W2_ROWS + 4 * KIB)
+        z_weave(1, *HALVES[1], nc.vector.tensor_copy, AT_Z_WOVEN)
+        w3_quantise(1)
 
         for m0, m1 in reversed(HALVES):
             z_quantise(1, m0, m1)

@@ -29,7 +29,9 @@ ACC_BANKS = 7
 EARLY_BANKS = 2
 EARLY_PICKS = 4
 
-V_AT, W1_AT, V2_AT = 0, S, S + H
+V_AT, W1_AT = 0, S
+V2_ROWS_AT = 64
+V2_PLANE_AT = (4, 8)
 
 HALVES = [(0, M // 2), (M // 2, M)]
 
@@ -39,10 +41,11 @@ AT_W2_BLOCK = 0
 AT_LAST_W2_RAW = AT_W2_BLOCK + 512
 AT_W1_SECOND = 8 * KIB + 512
 AT_W2_ROWS = 11 * KIB
-AT_TAB2 = (27 * KIB, 35 * KIB)
+AT_V2_PLANES = 27 * KIB
+AT_TAB2 = (27 * KIB + 512, 35 * KIB + 512)
 AT_W1_CODES = 45 * KIB
 AT_V_CODES = 47 * KIB
-AT_V2_SCALES = AT_V_CODES - M // 2
+AT_V_SCALES = AT_V_CODES - S // 2
 AT_LAST_W2_CODES = 65 * KIB
 AT_Z_WOVEN = 61 * KIB
 AT_W3_ROUNDED = 68 * KIB
@@ -68,20 +71,22 @@ def tile_list_stemma_innovation_scores_kernel(
         tab_s = sbuf("tab_s", [P, T], U8)
         tab2_s = sbuf("tab2_s", [P, T2], U8)
         w1_s_raw = sbuf("w1_s_raw", [SCALE_ROWS, H], U8)
-        for rows, engine in ((tab_s, nc.vector), (tab2_s, nc.gpsimd)):
-            engine.memset(rows[32:64, :].bitcast(I32), 0)
-            engine.memset(rows[64:128, :].bitcast(I32), 0)
-        planes = [sbuf("planes%d" % a, [P, S + H + M], U8) for a in range(2)]
-        for a in range(2):
-            nc.gpsimd.memset(planes[a][:].bitcast(I32), 0)
+        nc.vector.memset(tab_s[32:64, :].bitcast(I32), 0)
+        nc.vector.memset(tab_s[64:128, :].bitcast(I32), 0)
+        planes = [sbuf("planes%d" % a, [P, S + H], U8) for a in range(2)]
+        for cleared in (planes[0][:], planes[1][:], tab2_s[:V2_ROWS_AT, :], tab2_s[V2_ROWS_AT + SCALE_ROWS :, :]):
+            nc.gpsimd.memset(cleared.bitcast(I32), 0)
 
         idx = lists.tile([P, S // LIST_ROWS], U16, name="idx")
         nc.sync.dma_start(idx[:], offs)
         nc.sync.dma_start(tab_s[:SCALE_ROWS, :].bitcast(I32), tab_scales.rearrange("a q t -> (a q) t").bitcast(I32))
+        nc.sync.dma_start(w1_s_raw[:].bitcast(I32), w1_scales.rearrange("a q c -> (a q) c").bitcast(I32))
         idx2 = lists.tile([P, M // LIST_ROWS], U16, name="idx2")
         nc.sync.dma_start(idx2[:], offs2)
-        nc.sync.dma_start(tab2_s[:SCALE_ROWS, :].bitcast(I32), tab2_scales.rearrange("a q t -> (a q) t").bitcast(I32))
-        nc.sync.dma_start(w1_s_raw[:].bitcast(I32), w1_scales.rearrange("a q c -> (a q) c").bitcast(I32))
+        nc.sync.dma_start(
+            tab2_s[V2_ROWS_AT : V2_ROWS_AT + SCALE_ROWS, :].bitcast(I32),
+            tab2_scales.rearrange("a q t -> (a q) t").bitcast(I32),
+        )
         p1 = lists.tile([P, M // LIST_ROWS], U16, name="p1")
         nc.sync.dma_start(p1[:], pos1)
         w1_raw = {}
@@ -99,22 +104,21 @@ def tile_list_stemma_innovation_scores_kernel(
             tab_w.append(sbuf("tab_w%d" % a, [P, T], I32, AT_TAB[a]))
             nc.sync.dma_start(tab_w[a][:], tab_words[a].rearrange("p t i -> p (t i)").bitcast(I32))
 
-        v_s = sbuf("v_s", [P, S], U8)
+        v_s = sbuf("v_s", [P, S], U8, AT_V_SCALES)
         nc.vector.tensor_copy(v_s[:], tab_s[:].indirect(idx[:]))
-        v2_s = sbuf("v2_s", [P, M], U8, AT_V2_SCALES)
-        nc.vector.tensor_copy(v2_s[:], tab2_s[:].indirect(idx2[:]))
         staged = planes[0][:SCALE_ROWS, :]
-        nc.vector.tensor_copy(staged[:, V_AT:W1_AT].bitcast(I32), v_s[:SCALE_ROWS, :].bitcast(I32))
         nc.vector.tensor_copy(
-            staged[:, W1_AT:V2_AT].bitcast(I32).rearrange("p (c t g e) -> p c t g e", t=PACK, g=BLOCKS, e=2),
+            staged[:, W1_AT:].bitcast(I32).rearrange("p (c t g e) -> p c t g e", t=PACK, g=BLOCKS, e=2),
             w1_s_raw[:].bitcast(I32).rearrange("p (c g t e) -> p c t g e", t=PACK, g=BLOCKS, e=2),
         )
-        nc.vector.tensor_copy(staged[:, V2_AT:].bitcast(I32), v2_s[:SCALE_ROWS, :].bitcast(I32))
+        nc.vector.tensor_copy(staged[:, V_AT:W1_AT].bitcast(I32), v_s[:SCALE_ROWS, :].bitcast(I32))
         for a in range(2):
             for u in range(1 - a, 4):
                 queue = nc.gpsimd if (a, u) == (0, 1) else nc.scalar
                 row = 16 * a + 4 * u
                 queue.dma_start(planes[a][32 * u : 32 * u + 4, :].bitcast(I32), staged[row : row + 4, :].bitcast(I32))
+        v2_s = sbuf("v2_s", [P, M], U8)
+        nc.vector.tensor_copy(v2_s[:], tab2_s[:].indirect(idx2[:]))
 
         w1_c = {}
 
@@ -156,6 +160,13 @@ def tile_list_stemma_innovation_scores_kernel(
         for a in range(2):
             tab2_w.append(sbuf("tab2_w%d" % a, [P, T2], I32, AT_TAB2[a]))
             nc.sync.dma_start(tab2_w[a][:], tab2_words[a].rearrange("p t i -> p (t i)").bitcast(I32))
+        v2_planes = sbuf("v2_planes", [P, M], U8, AT_V2_PLANES)
+        nc.gpsimd.memset(v2_planes[:].bitcast(I32), 0)
+        for a in range(2):
+            for u in range(4):
+                queue = nc.gpsimd if u == 0 else nc.sync
+                row, to = V2_ROWS_AT + 16 * a + 4 * u, 32 * u + V2_PLANE_AT[a]
+                queue.dma_start(v2_planes[to : to + 4, :].bitcast(I32), v2_s[row : row + 4, :].bitcast(I32))
         ident = sbuf("ident", [P, P], F32)
         make_identity(nc, ident[:])
 
@@ -231,7 +242,7 @@ def tile_list_stemma_innovation_scores_kernel(
                 lhsT=w2_c[c, a][:, P * t : P * (t + 1)].bitcast(FP8X4),
                 lhsT_scale=w2_s[c, a][:, P * t : P * (t + 1)],
                 rhs=v2_c[a][:].bitcast(FP8X4),
-                rhs_scale=planes[a][:, V2_AT : V2_AT + M],
+                rhs_scale=v2_planes[V2_PLANE_AT[a] :, :],
                 start=first, stop=not first,
             )
 

@@ -370,10 +370,8 @@ def tile_list_stemma_innovation_scores_kernel(
         for t in range(PACK):
             b_pass(0, t, 1)
             b_tanh(0, t)
-        turned = psum.tile([P, BANK], F32, name="turned")
-        nc.tensor.transpose(turned[:, :P], gain_rows[:], ident[:])
-        half_gain = sbuf("half_gain", [P, 2 * PACK], F32)
-        nc.vector.tensor_scalar(half_gain[:], turned[:, : 2 * PACK], 0.5, None, ALU.mult)
+        for t in range(PACK):
+            b_pass(1, t, 1)
         w2_rounded[1, 0] = sbuf("w2_rounded10", [P, PACK, P, PACK], BF16, AT_LAST_W2_ROUNDED)
         for u in range(2):
             nc.vector.tensor_copy(
@@ -382,13 +380,16 @@ def tile_list_stemma_innovation_scores_kernel(
             )
         w2_quantise(1, 0, AT_LAST_W2_CODES)
         for t in range(PACK):
-            for a in (1, 0):
-                b_pass(1, t, a)
+            b_pass(1, t, 0)
             b_tanh(1, t)
 
-        at_product = (AT_LAST_W2_RAW + 4 * KIB, AT_LAST_W2_ROUNDED, AT_LAST_W2_ROUNDED + 2 * KIB, AT_LAST_W2_RAW + 6 * KIB)
+        at_product = (AT_LAST_W2_RAW + 4 * KIB, AT_LAST_W2_ROUNDED + 64, AT_LAST_W2_ROUNDED + 2 * KIB + 64, AT_LAST_W2_RAW + 6 * KIB)
         for t in range(PACK):
             product(0, t, 0, M, at_product[t])
+        turned = psum.tile([P, BANK], F32, name="turned")
+        nc.tensor.transpose(turned[:, :P], gain_rows[:], ident[:])
+        half_gain = sbuf("half_gain", [P, 2 * PACK], F32, AT_LAST_W2_ROUNDED)
+        nc.vector.tensor_scalar(half_gain[:], turned[:, : 2 * PACK], 0.5, None, ALU.mult)
         for t in range(PACK):
             z_row(0, t, 0, M)
         z_weave(0, 0, M, nc.scalar.copy, AT_Z_WOVEN)

@@ -193,10 +193,11 @@ def tile_list_stemma_innovation_scores_kernel(
 
         def w2_round(c, a, at=None):
             w2_rounded[c, a] = sbuf("w2_rounded%d%d" % (c, a), [P, PACK, P, PACK], BF16, at)
-            nc.vector.tensor_copy(
-                w2_rounded[c, a][:].rearrange("p t (g e) i -> p t g e i", e=RUN),
-                w2_raw[c, a][:].rearrange("p i (g t e) -> p t g e i", t=PACK, e=RUN),
-            )
+            for v in range(2):
+                nc.vector.tensor_copy(
+                    w2_rounded[c, a][:].rearrange("p t (g v e) i -> p v t g i e", v=2, e=4)[:, v],
+                    w2_raw[c, a][:].rearrange("p i (g t v e) -> p v t g i e", t=PACK, v=2, e=4)[:, v],
+                )
 
         def w2_round_on_gpsimd(c, a):
             w2_rounded[c, a] = sbuf("w2_rounded%d%d" % (c, a), [P, PACK, P, PACK], BF16)
@@ -374,10 +375,11 @@ def tile_list_stemma_innovation_scores_kernel(
             b_pass(1, t, 1)
         w2_rounded[1, 0] = sbuf("w2_rounded10", [P, PACK, P, PACK], BF16, AT_LAST_W2_ROUNDED)
         for u in range(2):
-            nc.vector.tensor_copy(
-                w2_rounded[1, 0][:].rearrange("p t (u g e) i -> p u t g e i", u=2, e=RUN)[:, u],
-                last_raw[u][:].rearrange("p i (g t e) -> p t g e i", t=PACK, e=RUN),
-            )
+            for v in range(2):
+                nc.vector.tensor_copy(
+                    w2_rounded[1, 0][:].rearrange("p t (u g v e) i -> p u v t g i e", u=2, v=2, e=4)[:, u, v],
+                    last_raw[u][:].rearrange("p i (g t v e) -> p v t g i e", t=PACK, v=2, e=4)[:, v],
+                )
         w2_quantise(1, 0, AT_LAST_W2_CODES)
         for t in range(PACK):
             b_pass(1, t, 0)
@@ -399,13 +401,13 @@ def tile_list_stemma_innovation_scores_kernel(
         product(1, 0, 0, M)
         z_row(1, 0, 0, M)
         w3_round(0, nc.vector.tensor_copy, AT_W3_ROUNDED)
-        product(1, 1, 0, M, AT_W2_ROWS)
+        product(1, 1, 0, M)
         w3_quantise(0)
-        product(1, 2, 0, M, AT_W2_ROWS + 2 * KIB)
+        product(1, 2, 0, M)
         z_row(1, 1, 0, M, on_vector=True)
-        product(1, last, *HALVES[0], AT_W3_ROUNDED)
+        product(1, last, *HALVES[0])
         z_row(1, 2, 0, M, on_vector=True)
-        product(1, last, *HALVES[1], AT_W3_ROUNDED + KIB)
+        product(1, last, *HALVES[1])
         z_row(1, last, *HALVES[0], on_vector=True)
         z_quantise(0, 0, M)
         z_row(1, last, *HALVES[1], on_vector=True)

@@ -27,6 +27,7 @@ SCALE_ROWS = 32
 BLOCKS = 16
 ACC_BANKS = 7
 EARLY_BANKS = 2
+WARM_UP_PASSES = 5
 EARLY_PICKS = 4
 
 V_AT, W1_AT = 0, S
@@ -403,6 +404,13 @@ def tile_list_stemma_innovation_scores_kernel(
         w3_round(0, nc.vector.tensor_copy, AT_W3_ROUNDED)
         product(1, 1, 0, M)
         w3_quantise(0)
+        idle = psum.tile([P, BANK], F32, name="turned")
+        for k in range(WARM_UP_PASSES):
+            nc.tensor.matmul_mx(
+                out=idle[:], lhsT=w3_c[0][:, :P].bitcast(FP8X4), lhsT_scale=w3_s[0][:, :P],
+                rhs=w2_c[0, 0][:].bitcast(FP8X4), rhs_scale=w2_s[0, 0][:],
+                start=(k == 0), stop=(k == WARM_UP_PASSES - 1),
+            )
         product(1, 2, 0, M)
         z_row(1, 1, 0, M, on_vector=True)
         product(1, last, *HALVES[0])

@@ -42,7 +42,7 @@ AT_W2_BLOCK = 0
 AT_LAST_W2_RAW = AT_W2_BLOCK + 512
 AT_W1_SECOND = 8 * KIB + 512
 AT_W2_ROWS = 11 * KIB
-AT_V2_PLANES = 27 * KIB
+AT_V2_PLANES = (10 * KIB + 512, 27 * KIB)
 AT_TAB2 = (27 * KIB + 512, 35 * KIB + 512)
 AT_W1_CODES = 45 * KIB
 AT_V_CODES = 47 * KIB
@@ -161,13 +161,13 @@ def tile_list_stemma_innovation_scores_kernel(
         for a in range(2):
             tab2_w.append(sbuf("tab2_w%d" % a, [P, T2], I32, AT_TAB2[a]))
             nc.sync.dma_start(tab2_w[a][:], tab2_words[a].rearrange("p t i -> p (t i)").bitcast(I32))
-        v2_planes = sbuf("v2_planes", [P, M], U8, AT_V2_PLANES)
-        nc.gpsimd.memset(v2_planes[:].bitcast(I32), 0)
-        for a in range(2):
+        v2_planes = []
+        for a, queue in enumerate((nc.gpsimd, nc.sync)):
+            v2_planes.append(sbuf("v2_planes%d" % a, [P, M], U8, AT_V2_PLANES[a]))
+            nc.gpsimd.memset(v2_planes[a][:].bitcast(I32), 0)
             for u in range(4):
-                queue = nc.gpsimd if u == 0 else nc.sync
                 row, to = V2_ROWS_AT + 16 * a + 4 * u, 32 * u + V2_PLANE_AT[a]
-                queue.dma_start(v2_planes[to : to + 4, :].bitcast(I32), v2_s[row : row + 4, :].bitcast(I32))
+                queue.dma_start(v2_planes[a][to : to + 4, :].bitcast(I32), v2_s[row : row + 4, :].bitcast(I32))
         ident = sbuf("ident", [P, P], F32)
         make_identity(nc, ident[:])
 
@@ -244,7 +244,7 @@ def tile_list_stemma_innovation_scores_kernel(
                 lhsT=w2_c[c, a][:, P * t : P * (t + 1)].bitcast(FP8X4),
                 lhsT_scale=w2_s[c, a][:, P * t : P * (t + 1)],
                 rhs=v2_c[a][:].bitcast(FP8X4),
-                rhs_scale=v2_planes[V2_PLANE_AT[a] :, :],
+                rhs_scale=v2_planes[a][V2_PLANE_AT[a] :, :],
                 start=first, stop=not first,
             )
 
@@ -375,13 +375,20 @@ def tile_list_stemma_innovation_scores_kernel(
         for t in range(PACK):
             b_pass(1, t, 1)
         w2_rounded[1, 0] = sbuf("w2_rounded10", [P, PACK, P, PACK], BF16, AT_LAST_W2_ROUNDED)
+        w2_c[1, 0] = sbuf("w2_c10", [P, PASS], U32, AT_LAST_W2_CODES)
+        w2_s[1, 0] = sbuf("w2_s10", [P, PASS], U8)
+        woven = w2_rounded[1, 0][:].rearrange("p t (u g v e) i -> p u v t g i e", u=2, v=2, e=4)
         for u in range(2):
-            for v in range(2):
-                nc.vector.tensor_copy(
-                    w2_rounded[1, 0][:].rearrange("p t (u g v e) i -> p u v t g i e", u=2, v=2, e=4)[:, u, v],
-                    last_raw[u][:].rearrange("p i (g t v e) -> p v t g i e", t=PACK, v=2, e=4)[:, v],
-                )
-        w2_quantise(1, 0, AT_LAST_W2_CODES)
+            rows = last_raw[u][:].rearrange("p i (g t v e) -> p v t g i e", t=PACK, v=2, e=4)
+            for tiles in (slice(0, 2), slice(2, 4)) if u == 1 else (slice(0, 4),):
+                for v in range(2):
+                    nc.vector.tensor_copy(woven[:, u, v, tiles], rows[:, v, tiles])
+        for t0 in range(0, PACK, 2):
+            cols = slice(P * t0, P * (t0 + 2))
+            nc.vector.quantize_mx(
+                out=w2_c[1, 0][:, cols].bitcast(FP8X4), scales=w2_s[1, 0][:, cols],
+                in_=w2_rounded[1, 0][:, t0 : t0 + 2].rearrange("p t m i -> p (t m i)"),
+            )
         for t in range(PACK):
             b_pass(1, t, 0)
             b_tanh(1, t)

@@ -27,7 +27,6 @@ SCALE_ROWS = 32
 BLOCKS = 16
 ACC_BANKS = 7
 EARLY_BANKS = 2
-WARM_UP_PASSES = 5
 EARLY_PICKS = 4
 
 V_AT, W1_AT = 0, S
@@ -411,13 +410,6 @@ def tile_list_stemma_innovation_scores_kernel(
         w3_round(0, nc.vector.tensor_copy, AT_W3_ROUNDED)
         product(1, 1, 0, M)
         w3_quantise(0)
-        idle = psum.tile([P, BANK], F32, name="turned")
-        for k in range(WARM_UP_PASSES):
-            nc.tensor.matmul_mx(
-                out=idle[:], lhsT=w3_c[0][:, :P].bitcast(FP8X4), lhsT_scale=w3_s[0][:, :P],
-                rhs=w2_c[0, 0][:].bitcast(FP8X4), rhs_scale=w2_s[0, 0][:],
-                start=(k == 0), stop=(k == WARM_UP_PASSES - 1),
-            )
         product(1, 2, 0, M)
         z_row(1, 1, 0, M, on_vector=True)
         product(1, last, *HALVES[0])

from contextlib import ExitStack

import concourse.mybir as mybir
from concourse.masks import make_identity

K, T, T2, H, S, M, N = 1024, 4096, 2048, 1024, 1024, 512, 256
FLOPS = 2 * K * H * S + 2 * K * H * M + 2 * H * N * M

F32 = mybir.dt.float32
BF16 = mybir.dt.bfloat16
I32 = mybir.dt.int32
U32 = mybir.dt.uint32
U16 = mybir.dt.uint16
U8 = mybir.dt.uint8
FP8X4 = mybir.dt.float8_e4m3fn_x4
FP4X4 = mybir.dt.float4_e2m1fn_x4
ACT = mybir.ActivationFunctionType
ALU = mybir.AluOpType

P = 128
PACK = 4
PASS = P * PACK
RUN = 8
BANK = 512
LIST_ROWS = 16
SCALE_ROWS = 32
BLOCKS = 16
ACC_BANKS = 7
EARLY_BANKS = 2
EARLY_PICKS = 4

V_AT, W1_AT = 0, S
V2_ROWS_AT = 64
V2_PLANE_AT = (4, 8)

HALVES = [(0, M // 2), (M // 2, M)]

KIB = 1024
AT_TAB = (4 * KIB, 27 * KIB)
AT_W2_BLOCK = 0
AT_LAST_W2_RAW = AT_W2_BLOCK + 512
AT_W1_SECOND = 8 * KIB + 512
AT_W2_ROWS = 11 * KIB
AT_V2_PLANES = (10 * KIB + 512, 27 * KIB)
AT_TAB2 = (27 * KIB + 512, 35 * KIB + 512)
AT_W1_CODES = 45 * KIB
AT_V_CODES = 47 * KIB
AT_V_SCALES = AT_V_CODES - S // 2
AT_LAST_W2_CODES = 65 * KIB
AT_Z_WOVEN = 61 * KIB
AT_W3_ROUNDED = 68 * KIB
AT_LAST_W2_ROUNDED = 55 * KIB


def tile_list_stemma_innovation_scores_kernel(
    tc, tab_words, tab_scales, offs, w1_words, w1_scales, pos1,
    tab2_words, tab2_scales, offs2, w2, gain, w3, out,
):
    nc = tc.nc
    with ExitStack() as ctx:
        lists = ctx.enter_context(tc.tile_pool(name="lists", bufs=1))
        keep = ctx.enter_context(tc.tile_pool(name="keep", bufs=1))
        reused = ctx.enter_context(tc.tile_pool(name="reused", bufs=1))
        psum = ctx.enter_context(tc.psum_pool(name="psum", bufs=1))

        def sbuf(name, shape, dtype, at=None):
            if at is None:
                return keep.tile(shape, dtype, name=name, align_bytes=64)
            return reused.tile(shape, dtype, name=name, align_bytes=64, offset=at)

        tab_s = sbuf("tab_s", [P, T], U8)
        tab2_s = sbuf("tab2_s", [P, T2], U8)
        w1_s_raw = sbuf("w1_s_raw", [SCALE_ROWS, H], U8)
        nc.vector.memset(tab_s[32:64, :].bitcast(I32), 0)
        nc.vector.memset(tab_s[64:128, :].bitcast(I32), 0)
        planes = [sbuf("planes%d" % a, [P, S + H], U8) for a in range(2)]
        for cleared in (planes[0][:], planes[1][:], tab2_s[:V2_ROWS_AT, :], tab2_s[V2_ROWS_AT + SCALE_ROWS :, :]):
            nc.gpsimd.memset(cleared.bitcast(I32), 0)

        idx = lists.tile([P, S // LIST_ROWS], U16, name="idx")
        nc.sync.dma_start(idx[:], offs)
        nc.sync.dma_start(tab_s[:SCALE_ROWS, :].bitcast(I32), tab_scales.rearrange("a q t -> (a q) t").bitcast(I32))
        nc.sync.dma_start(w1_s_raw[:].bitcast(I32), w1_scales.rearrange("a q c -> (a q) c").bitcast(I32))
        idx2 = lists.tile([P, M // LIST_ROWS], U16, name="idx2")
        nc.sync.dma_start(idx2[:], offs2)
        nc.sync.dma_start(
            tab2_s[V2_ROWS_AT : V2_ROWS_AT + SCALE_ROWS, :].bitcast(I32),
            tab2_scales.rearrange("a q t -> (a q) t").bitcast(I32),
        )
        p1 = lists.tile([P, M // LIST_ROWS], U16, name="p1")
        nc.sync.dma_start(p1[:], pos1)
        w1_raw = {}

        def w1_load(c, at=None):
            w1_raw[c] = sbuf("w1_raw%d" % c, [P, 2 * H], U8, at)
            nc.sync.dma_start(
                w1_raw[c][:].bitcast(I32).rearrange("p (a c) -> p a c", a=2),
                w1_words.bitcast(I32).rearrange("a p c -> p a c")[:, :, H // 4 * c : H // 4 * (c + 1)],
            )

        w1_load(0)
        tab_w = []
        for a in range(2):
            tab_w.append(sbuf("tab_w%d" % a, [P, T], I32, AT_TAB[a]))
            nc.sync.dma_start(tab_w[a][:], tab_words[a].rearrange("p t i -> p (t i)").bitcast(I32))

        v_s = sbuf("v_s", [P, S], U8, AT_V_SCALES)
        nc.vector.tensor_copy(v_s[:], tab_s[:].indirect(idx[:]))
        staged = planes[0][:SCALE_ROWS, :]
        nc.vector.tensor_copy(
            staged[:, W1_AT:].bitcast(I32).rearrange("p (c t g e) -> p c t g e", t=PACK, g=BLOCKS, e=2),
            w1_s_raw[:].bitcast(I32).rearrange("p (c g t e) -> p c t g e", t=PACK, g=BLOCKS, e=2),
        )
        nc.vector.tensor_copy(staged[:, V_AT:W1_AT].bitcast(I32), v_s[:SCALE_ROWS, :].bitcast(I32))
        for a in range(2):
            for u in range(1 - a, 4):
                queue = nc.gpsimd if (a, u) == (0, 1) else nc.scalar
                row = 16 * a + 4 * u
                queue.dma_start(planes[a][32 * u : 32 * u + 4, :].bitcast(I32), staged[row : row + 4, :].bitcast(I32))
        v2_s = sbuf("v2_s", [P, M], U8)
        nc.vector.tensor_copy(v2_s[:], tab2_s[:].indirect(idx2[:]))

        w1_c = {}

        def w1_order(c, at=None):
            w1_c[c] = sbuf("w1_c%d" % c, [P, 2 * H], U8, at)
            nc.vector.tensor_copy(
                w1_c[c][:].bitcast(I32).rearrange("p (a t g e) -> p a t g e", t=PACK, g=BLOCKS, e=4),
                w1_raw[c][:].bitcast(I32).rearrange("p (a g t e) -> p a t g e", t=PACK, g=BLOCKS, e=4),
            )

        w1_order(0, AT_W1_CODES)

        v_c0 = sbuf("v_c0", [P, S], U32, AT_V_CODES)
        nc.vector.tensor_copy(v_c0[:], tab_w[0][:].bitcast(U32).indirect(idx[:]))
        v_c = {}
        for h in range(2):
            v_c[0, h] = v_c0[:, BANK * h : BANK * (h + 1)]
        for h in range(2):
            gathered = sbuf("v_c1%d" % h, [P, BANK], U32)
            entries = idx[:, BANK * h // LIST_ROWS : BANK * (h + 1) // LIST_ROWS]
            nc.vector.tensor_copy(gathered[:], tab_w[1][:].bitcast(U32).indirect(entries))
            v_c[1, h] = gathered[:]

        w2_raw = {}

        def w2_load_block(c):
            w2_raw[c, 0] = sbuf("w2_raw%d0" % c, [P, PACK, PASS], F32, AT_W2_BLOCK)
            nc.sync.dma_start(
                w2_raw[c, 0][:], w2[:PASS, PASS * c : PASS * (c + 1)].rearrange("(p i) r -> p i r", i=PACK)
            )

        w2_load_block(0)
        w1_load(1, AT_W1_SECOND)
        w2_rows = sbuf("w2_rows", [P, PACK, H], F32, AT_W2_ROWS)
        nc.sync.dma_start(w2_rows[:], w2[PASS:, :].rearrange("(p i) r -> p i r", i=PACK))
        for c in range(2):
            w2_raw[c, 1] = w2_rows[:, :, PASS * c : PASS * (c + 1)]
        tab2_w = []
        for a in range(2):
            tab2_w.append(sbuf("tab2_w%d" % a, [P, T2], I32, AT_TAB2[a]))
            nc.sync.dma_start(tab2_w[a][:], tab2_words[a].rearrange("p t i -> p (t i)").bitcast(I32))
        v2_planes = []
        for a, queue in enumerate((nc.gpsimd, nc.sync)):
            v2_planes.append(sbuf("v2_planes%d" % a, [P, M], U8, AT_V2_PLANES[a]))
            nc.gpsimd.memset(v2_planes[a][:].bitcast(I32), 0)
            for u in range(4):
                row, to = V2_ROWS_AT + 16 * a + 4 * u, 32 * u + V2_PLANE_AT[a]
                queue.dma_start(v2_planes[a][to : to + 4, :].bitcast(I32), v2_s[row : row + 4, :].bitcast(I32))
        ident = sbuf("ident", [P, P], F32)
        make_identity(nc, ident[:])

        tanh_x1 = {}

        def x1_bank(c, t, h, at=None):
            if h == 0:
                tanh_x1[c, t] = sbuf("tanh_x1_%d%d" % (c, t), [P, S], F32, at)
            col = PASS * c + P * t
            acc = psum.tile([P, BANK], F32, name="acc", bufs=ACC_BANKS)
            k_passes = (0, 1) if (c, h) == (0, 0) and t < EARLY_BANKS else (1, 0)
            for a in k_passes:
                nc.tensor.matmul_mx(
                    out=acc[:],
                    lhsT=w1_c[c][:, 2 * (PASS * a + P * t) : 2 * (PASS * a + P * (t + 1))].bitcast(FP4X4),
                    lhsT_scale=planes[a][:, W1_AT + col : W1_AT + col + P],
                    rhs=v_c[a, h].bitcast(FP8X4),
                    rhs_scale=planes[a][:, V_AT + BANK * h : V_AT + BANK * (h + 1)],
                    start=(a == k_passes[0]), stop=(a == k_passes[1]),
                )
            nc.scalar.activation(tanh_x1[c, t][:, BANK * h : BANK * (h + 1)], acc[:], ACT.Tanh, scale=0.5)

        w2_rounded, w2_c, w2_s = {}, {}, {}

        def w2_round(c, a, at=None):
            w2_rounded[c, a] = sbuf("w2_rounded%d%d" % (c, a), [P, PACK, P, PACK], BF16, at)
            for v in range(2):
                nc.vector.tensor_copy(
                    w2_rounded[c, a][:].rearrange("p t (g v e) i -> p v t g i e", v=2, e=4)[:, v],
                    w2_raw[c, a][:].rearrange("p i (g t v e) -> p v t g i e", t=PACK, v=2, e=4)[:, v],
                )

        def w2_round_on_gpsimd(c, a):
            w2_rounded[c, a] = sbuf("w2_rounded%d%d" % (c, a), [P, PACK, P, PACK], BF16)
            for t in range(PACK):
                nc.gpsimd.tensor_scalar(
                    w2_rounded[c, a][:, t].rearrange("p (g e) i -> p g e i", e=RUN),
                    w2_raw[c, a][:].rearrange("p i (g t e) -> p t g e i", t=PACK, e=RUN)[:, t],
                    1.0, 0.0, ALU.mult, ALU.add,
                )

        def w2_round_on_scalar(c, a):
            w2_rounded[c, a] = sbuf("w2_rounded%d%d" % (c, a), [P, PACK, P, PACK], BF16)
            for t in range(PACK):
                nc.scalar.copy(
                    w2_rounded[c, a][:, t].rearrange("p (g u e) i -> p g u i e", u=2, e=4),
                    w2_raw[c, a][:].rearrange("p i (g t u e) -> p t g u i e", t=PACK, u=2, e=4)[:, t],
                )

        def w2_quantise(c, a, at=None):
            w2_c[c, a] = sbuf("w2_c%d%d" % (c, a), [P, PASS], U32, at)
            w2_s[c, a] = sbuf("w2_s%d%d" % (c, a), [P, PASS], U8)
            nc.vector.quantize_mx(
                out=w2_c[c, a][:].bitcast(FP8X4), scales=w2_s[c, a][:],
                in_=w2_rounded[c, a][:].rearrange("p t m i -> p (t m i)"),
            )

        v2_c = []

        def v2_gather(a):
            v2_c.append(sbuf("v2_c%d" % a, [P, M], U32))
            nc.vector.tensor_copy(v2_c[a][:], tab2_w[a][:].bitcast(U32).indirect(idx2[:]))

        tanh_b = {}

        b_acc = {}

        def b_pass(c, t, a):
            first = (c, t) not in b_acc
            if first:
                b_acc[c, t] = psum.tile([P, BANK], F32, name="acc", bufs=ACC_BANKS)
            nc.tensor.matmul_mx(
                out=b_acc[c, t][:],
                lhsT=w2_c[c, a][:, P * t : P * (t + 1)].bitcast(FP8X4),
                lhsT_scale=w2_s[c, a][:, P * t : P * (t + 1)],
                rhs=v2_c[a][:].bitcast(FP8X4),
                rhs_scale=v2_planes[a][V2_PLANE_AT[a] :, :],
                start=first, stop=not first,
            )

        def b_tanh(c, t):
            tanh_b[c, t] = sbuf("tanh_b%d%d" % (c, t), [P, M], F32)
            nc.scalar.activation(tanh_b[c, t][:], b_acc[c, t][:], ACT.Tanh, scale=-0.5)

        picked = {}

        def pick(c, t):
            picked[c, t] = sbuf("picked%d%d" % (c, t), [P, M], F32)
            nc.vector.tensor_copy(picked[c, t][:], tanh_x1[c, t][:].indirect(p1[:]))

        products = {}

        def product(c, t, m0, m1, at=None):
            products[c, t, m0] = sbuf("product%d%d_%d" % (c, t, m0), [P, m1 - m0], F32, at)
            if (c, t) in picked:
                exemplar = picked[c, t][:, m0:m1]
            else:
                exemplar = tanh_x1[c, t][:].indirect(p1[:, m0 // LIST_ROWS : m1 // LIST_ROWS])
            nc.vector.tensor_tensor(products[c, t, m0][:], exemplar, tanh_b[c, t][:, m0:m1], ALU.mult)

        z_rows = {}

        def z_row(c, t, m0, m1, on_vector=False):
            if c not in z_rows:
                z_rows[c] = sbuf("z_rows%d" % c, [P, PACK, M], BF16, AT_TAB2[0] if c == 0 else None)
            factor = half_gain[:, PACK * c + t : PACK * c + t + 1]
            if on_vector:
                nc.vector.tensor_scalar(z_rows[c][:, t, m0:m1], products[c, t, m0][:], factor, factor, ALU.mult, ALU.add)
            else:
                nc.scalar.activation(
                    z_rows[c][:, t, m0:m1], products[c, t, m0][:], ACT.Identity, scale=factor, bias=factor
                )

        z_c = [sbuf("z_c%d" % c, [P, M], U32) for c in range(2)]
        z_s = [sbuf("z_s%d" % c, [P, M], U8) for c in range(2)]

        z_woven = {}

        def z_weave(c, m0, m1, copy, at=None):
            z_woven[c, m0] = sbuf("z_woven%d_%d" % (c, m0), [P, m1 - m0, PACK], BF16, at)
            copy(
                z_woven[c, m0][:].rearrange("p (f i) t -> p f t i", i=4),
                z_rows[c][:, :, m0:m1].rearrange("p t (f i) -> p f t i", i=4),
            )

        def z_quantise(c, m0, m1):
            nc.vector.quantize_mx(
                out=z_c[c][:, m0:m1].bitcast(FP8X4), scales=z_s[c][:, m0:m1],
                in_=z_woven[c, m0][:].rearrange("p m t -> p (m t)"),
            )

        w3_rounded, w3_c, w3_s = {}, {}, {}

        def w3_round(c, copy, at):
            w3_rounded[c] = sbuf("w3_rounded%d" % c, [P, N, PACK], BF16, at)
            copy(
                w3_rounded[c][:].rearrange("p (f i) t -> p f t i", i=4),
                w3_raw[c][:].rearrange("p t (f i) -> p f t i", i=4),
            )

        def w3_quantise(c):
            w3_c[c] = sbuf("w3_c%d" % c, [P, N], U32)
            w3_s[c] = sbuf("w3_s%d" % c, [P, N], U8)
            nc.vector.quantize_mx(
                out=w3_c[c][:].bitcast(FP8X4), scales=w3_s[c][:], in_=w3_rounded[c][:].rearrange("p n t -> p (n t)")
            )

        def scores(acc, c, n, m0, m1):
            cols = slice(P * n, P * (n + 1))
            nc.tensor.matmul_mx(
                out=acc,
                lhsT=w3_c[c][:, cols].bitcast(FP8X4),
                lhsT_scale=w3_s[c][:, cols],
                rhs=z_c[c][:, m0:m1].bitcast(FP8X4),
                rhs_scale=z_s[c][:, m0:m1],
                start=(c == 0), stop=(c == 1),
            )

        for t0 in range(0, PACK, 2):
            for h in range(2):
                for t in (t0, t0 + 1):
                    x1_bank(0, t, h)

        w2_round(0, 0)
        w1_order(1)
        last_raw = []
        for u in range(2):
            last_raw.append(sbuf("last_raw%d" % u, [P, PACK, PASS // 2], F32, AT_LAST_W2_RAW + 4 * KIB * u))
            cols = slice(PASS + PASS // 2 * u, PASS + PASS // 2 * (u + 1))
            nc.sync.dma_start(last_raw[u][:], w2[:PASS, cols].rearrange("(p i) r -> p i r", i=PACK))
        gain_rows = sbuf("gain_rows", [P, P], F32, AT_W2_BLOCK)
        nc.gpsimd.memset(gain_rows[:], 0.0)
        for c in range(2):
            nc.sync.dma_start(
                gain_rows[PACK * c : PACK * (c + 1), :].rearrange("t (g e) -> t g e", e=RUN),
                gain.rearrange("(c g t e) -> c t g e", c=2, t=PACK, e=RUN)[c],
            )
        w2_quantise(0, 0)
        for t in range(EARLY_PICKS):
            pick(0, t)
        for t in range(2):
            for h in range(2):
                x1_bank(1, t, h)
        w2_round_on_scalar(0, 1)
        w2_round_on_gpsimd(1, 1)
        w3_rows = w3.rearrange("(c g t e) n -> c t g e n", c=2, t=PACK, e=RUN)
        w3_raw = []
        for c in range(2):
            w3_raw.append(sbuf("w3_raw%d" % c, [P, PACK, N], F32, AT_W2_ROWS + 4 * KIB * c))
            for t in range(PACK):
                nc.sync.dma_start(w3_raw[c][:, t, :], w3_rows[c, t])
        v2_gather(0)
        w2_quantise(0, 1, AT_TAB2[0] + 4 * KIB)
        w2_quantise(1, 1, AT_TAB2[0] + 6 * KIB)
        v2_gather(1)

        for t in range(2, PACK):
            for h in range(2):
                x1_bank(1, t, h, AT_W2_ROWS + 4 * KIB * t)
        for t in range(PACK):
            b_pass(0, t, 0)
        for t in range(PACK):
            b_pass(0, t, 1)
            b_tanh(0, t)
        for t in range(PACK):
            b_pass(1, t, 1)
        w2_rounded[1, 0] = sbuf("w2_rounded10", [P, PACK, P, PACK], BF16, AT_LAST_W2_ROUNDED)
        w2_c[1, 0] = sbuf("w2_c10", [P, PASS], U32, AT_LAST_W2_CODES)
        w2_s[1, 0] = sbuf("w2_s10", [P, PASS], U8)
        woven = w2_rounded[1, 0][:].rearrange("p t (u g v e) i -> p u v t g i e", u=2, v=2, e=4)
        for u in range(2):
            rows = last_raw[u][:].rearrange("p i (g t v e) -> p v t g i e", t=PACK, v=2, e=4)
            for tiles in (slice(0, 2), slice(2, 4)) if u == 1 else (slice(0, 4),):
                for v in range(2):
                    nc.vector.tensor_copy(woven[:, u, v, tiles], rows[:, v, tiles])
        for t0 in range(0, PACK, 2):
            cols = slice(P * t0, P * (t0 + 2))
            nc.vector.quantize_mx(
                out=w2_c[1, 0][:, cols].bitcast(FP8X4), scales=w2_s[1, 0][:, cols],
                in_=w2_rounded[1, 0][:, t0 : t0 + 2].rearrange("p t m i -> p (t m i)"),
            )
        for t in range(PACK):
            b_pass(1, t, 0)
            b_tanh(1, t)

        at_product = (AT_LAST_W2_RAW + 4 * KIB, AT_LAST_W2_ROUNDED + 64, AT_LAST_W2_ROUNDED + 2 * KIB + 64, AT_LAST_W2_RAW + 6 * KIB)
        for t in range(PACK):
            product(0, t, 0, M, at_product[t])
        turned = psum.tile([P, BANK], F32, name="turned")
        nc.tensor.transpose(turned[:, :P], gain_rows[:], ident[:])
        half_gain = sbuf("half_gain", [P, 2 * PACK], F32, AT_LAST_W2_ROUNDED)
        nc.vector.tensor_scalar(half_gain[:], turned[:, : 2 * PACK], 0.5, None, ALU.mult)
        for t in range(PACK):
            z_row(0, t, 0, M)
        z_weave(0, 0, M, nc.scalar.copy, AT_Z_WOVEN)
        w3_round(1, nc.scalar.copy, AT_LAST_W2_CODES)

        last = PACK - 1
        product(1, 0, 0, M)
        z_row(1, 0, 0, M)
        w3_round(0, nc.vector.tensor_copy, AT_W3_ROUNDED)
        product(1, 1, 0, M)
        w3_quantise(0)
        product(1, 2, 0, M)
        z_row(1, 1, 0, M, on_vector=True)
        product(1, last, *HALVES[0])
        z_row(1, 2, 0, M, on_vector=True)
        product(1, last, *HALVES[1])
        z_row(1, last, *HALVES[0], on_vector=True)
        z_quantise(0, 0, M)
        z_row(1, last, *HALVES[1], on_vector=True)
        banks = {}
        for m0, m1 in reversed(HALVES):
            for n in range(2):
                banks[m0, n] = psum.tile([P, BANK], F32, name="acc", bufs=ACC_BANKS)
                scores(banks[m0, n][:, : m1 - m0], 0, n, m0, m1)
        z_weave(1, *HALVES[0], nc.scalar.copy, AT_W2_ROWS + 4 * KIB)
        z_weave(1, *HALVES[1], nc.vector.tensor_copy, AT_Z_WOVEN)
        w3_quantise(1)

        for m0, m1 in reversed(HALVES):
            z_quantise(1, m0, m1)
            for n in range(2):
                scores(banks[m0, n][:, : m1 - m0], 1, n, m0, m1)
        for m0, m1 in reversed(HALVES):
            for n, copy in enumerate((nc.scalar.copy, nc.vector.tensor_copy)):
                done = sbuf("done%d_%d" % (m0, n), [P, m1 - m0], F32)
                copy(done[:], banks[m0, n][:, : m1 - m0])
                nc.sync.dma_start(out[P * n : P * (n + 1), m0:m1], done[:])
